import numpy as np, ml_dtypes
CORES = [10,34,74,98]
N = 4
import mx_ref
BF = ml_dtypes.bfloat16
def entries(a):
    return np.ascontiguousarray(a.T).reshape(-1)
def table(e):
    return np.ascontiguousarray(np.reshape(e, (-1, 16)).T).astype(np.int32)
def gentries(a):
    return np.ascontiguousarray(a.reshape(8, 16, -1).transpose(0, 2, 1)).reshape(8, -1)
def gtable(e):
    e = np.asarray(e); return np.ascontiguousarray(e.reshape(8, -1, 16).transpose(0, 2, 1)).reshape(128, -1).astype(np.int32)
def tile(rs):
    return np.stack(rs, axis=2).reshape(128, -1).astype(BF)
def cut(t, i, w=512):
    return t[:, w * i:w * i + w]
def f(rng, *shape):
    return mx_ref.flush((rng.standard_normal(shape, dtype=np.float32) * np.exp2(rng.integers(-2, 3, shape[:-1] + (1,)))).astype(BF))
def wide(rng, *shape, cols=0):
    v = rng.standard_normal(shape, dtype=np.float32) * np.exp2(rng.integers(-12, 13, shape)).astype(np.float32)
    if cols: v *= np.repeat(np.exp2(rng.integers(-cols, cols + 1, shape[:-2] + (1, shape[-1] // 4))) * (rng.random(shape[:-2] + (1, shape[-1] // 4)) > 0.0625), 4, axis=-1).astype(np.float32)
    return mx_ref.flush(v.astype(BF))
T, CAPP, P = 512, 96, 256
SL = N * CAPP
G = 8
def pieces(rng, how):
    if how == "ones": n = np.ones((G, SL), int)
    elif how == "full":
        n = T - rng.integers(0, 8, (G, SL)); n[:, ::4] = T
    elif how == "powers":
        k = [1 << i for i in range(T.bit_length())]; k = sorted(set(k + [i + 1 for i in k if i < T]))
        n = rng.permuted(np.tile(np.resize(k, SL), (G, 1)), axis=1)
    else: n = np.where(rng.random((G, SL)) < 0.5, rng.integers(1, T + 1, (G, SL)), np.clip(np.exp2(rng.uniform(0, T.bit_length() - 1, (G, SL))).astype(int), 1, T))
    s = rng.integers(0, T - n + 1)
    if how == "full": s[:] = 0
    if how == "nested":
        for g in range(G):
            for r in range(N):
                m = rng.integers(0, T)
                b = np.sort(rng.choice(rng.integers(0, m + 1, 16), CAPP)); e = np.sort(rng.choice(rng.integers(m, T, 16), CAPP))[::-1]
                k = r * CAPP + rng.permutation(CAPP); s[g, k] = b; n[g, k] = e - b + 1
    return s, n
def lists(rng, how="any", every=False):
    held = np.zeros((N, N, CAPP), bool)
    for r in range(N):
        n = rng.integers(0, CAPP + 1, N); n[(r + rng.integers(1, N)) % N] = CAPP
        for q in range(N): held[q, r, rng.permutation(CAPP)[:CAPP if every else n[q]]] = True
    d = {"lo": [], "ln": [], "pf": [], "pg": []}
    for q in range(N):
        s, n = pieces(rng, how); e = ~held[q].reshape(-1)
        s[:, e] = -1; n[:, e] = 0
        d["lo"].append(gtable(s)); d["ln"].append(gtable(n))
    who = rng.permutation(N)
    for r in range(N):
        k = rng.permutation(np.flatnonzero(held[:, r]))
        first = rng.permutation(np.resize(k, P))
        second = np.where(rng.random(P) < 0.25, -1, rng.choice(k, P))
        if how == "ones":
            if r == who[0]:
                first[rng.permutation(P)[:P // 2]] = k[0]; second[rng.permutation(P)[:P // 2]] = k[0]
            if r == who[1]: second[:] = -1
            if r == who[2]: second = rng.choice(k, P)
        d["pf"].append(table(first))
        d["pg"].append(table(second))
    return {k: np.stack(t) for k, t in d.items()}
def setup_inputs(rng):
    return {"x": f(rng, N, 128, 4 * T), "a": f(rng, N, 128, 2048), "u": f(rng, N, 128, 512), "v": f(rng, N, 128, 512), **lists(rng)}
def setup_inputs_ones(rng):
    return {**setup_inputs(rng), **lists(rng, "ones")}
def setup_inputs_full(rng):
    return {**setup_inputs(rng), **lists(rng, "full", True)}
def setup_inputs_powers(rng):
    return {**setup_inputs(rng), **lists(rng, "powers", True)}
def setup_inputs_nested(rng):
    return {**setup_inputs(rng), **lists(rng, "nested", True)}
def setup_inputs_spread(rng):
    d = setup_inputs(rng); d["x"] = wide(rng, N, 128, 4 * T, cols=8); return d
def check_inputs(d):
    b = []; held = []
    for q in range(N):
        s, n = gentries(d["lo"][q]).reshape(G, -1), gentries(d["ln"][q]).reshape(G, -1)
        e = s == -1; held.append(~e[0])
        if s.min() < -1 or s.max() >= T or (e != e[:1]).any(): b.append("lo")
        if (n[e] != 0).any() or (n[~e] < 1).any() or (n[~e] > T - s[~e]).any(): b.append("ln")
    for r in range(N):
        h = np.concatenate([held[q][r * CAPP:r * CAPP + CAPP] for q in range(N)])
        for k, least in (("pf", 0), ("pg", -1)):
            j = entries(d[k][r])
            if j.min() < least or j.max() >= SL or not h[j[(j >= 0) & (j < SL)]].all(): b.append(k)
    return b
def reference(x, a, u, v, lo, ln, pf, pg):
    sent = []
    for q in range(N):
        X = mx_ref.quantize(x[q])
        Z = np.stack([mx_ref.matmul(mx_ref.quantize(np.ascontiguousarray(cut(a[q], i))), X) for i in range(4)])
        h = np.maximum(Z, np.float32(0)) * np.float32(0.05)
        s, n = gentries(lo[q]), gentries(ln[q])
        R = np.zeros((4, 128, SL), np.float32)
        for k in range(SL):
            for g in range(8):
                if n[g, k]: R[:, 16 * g:16 * g + 16, k] = h[:, 16 * g:16 * g + 16, s[g, k]:s[g, k] + n[g, k]].max(axis=2)
        sent.append([mx_ref.quantize(np.ascontiguousarray(tile([R[i][:, CAPP * r:CAPP * r + CAPP] for i in range(4)]))) for r in range(N)])
    y = np.zeros((N, 128, P), np.float32)
    for r in range(N):
        V, U = mx_ref.quantize(v[r]), mx_ref.quantize(u[r])
        zv = np.concatenate([mx_ref.matmul(V, sent[q][r]) for q in range(N)], axis=1)
        zu = np.concatenate([mx_ref.matmul(U, sent[q][r]) for q in range(N)], axis=1)
        first, second = entries(pf[r]), entries(pg[r])
        y[r] = zv[:, first]
        two = second >= 0
        y[r][:, two] += zu[:, second[two]]
    return {"y": y}

@@ -1,0 +1,424 @@
+from concourse.bass import DstId, RemoteDMATransfer, IndirectOffsetOnAxis
+from concourse.mybir import dt, AluOpType, ActivationFunctionType
+
+A = AluOpType
+F = ActivationFunctionType
+N = 4
+CAPP = 96
+P = 256
+SL = N * CAPP
+X = 512
+LV = (2, 4)
+P16, P4, H0, S4, S16, NT = 0, 1, 2, 3, 4, 5
+PT = (P4, P16)
+ST = (S4, S16)
+NB = X // 16
+RW = 2 * NB
+NR = 35
+CROW = 32
+LEFT, MID, RIGHT = 0, 1, 2
+CUTS = ((0, 2 * CAPP), (2 * CAPP, 3 * CAPP), (3 * CAPP, SL))
+ALL, EARLY, REST = (0, SL), CUTS[0], (2 * CAPP, SL)
+
+SCRATCH = {
+    "xs": ("sbuf", [128, 2048], "bfloat16"),
+    "ab": ("sbuf", [128, 2048], "bfloat16"),
+    "uv": ("sbuf", [128, 1024], "bfloat16"),
+    "xq": ("sbuf", [128, 512], "float8_e4m3fn_x4"),
+    "xc": ("sbuf", [128, 512], "uint8"),
+    "aq": ("sbuf", [128, 512], "float8_e4m3fn_x4"),
+    "ac": ("sbuf", [128, 512], "uint8"),
+    "uvq": ("sbuf", [128, 256], "float8_e4m3fn_x4"),
+    "uvc": ("sbuf", [128, 256], "uint8"),
+    "ps": ("psum", [128, 4096], "float32"),
+    "tw": ("sbuf", [128, 4 * NT * X], "bfloat16"),
+    "bm": ("sbuf", [128, 4 * RW], "bfloat16"),
+    "bt": ("sbuf", [128, 2 * NR * RW], "bfloat16"),
+    "mk": ("sbuf", [128, 2 * X], "bfloat16"),
+    "mz": ("sbuf", [128, 5 * NB], "bfloat16"),
+    "mi": ("sbuf", [128, 2 * SL], "bfloat16"),
+    "one": ("sbuf", [128, 3 * SL], "bfloat16"),
+    "m3": ("sbuf", [128, 3 * SL], "bfloat16"),
+    "lnb": ("sbuf", [128, 24], "int32"),
+    "lob": ("sbuf", [128, 24], "int32"),
+    "wt": ("sbuf", [128, 2, 2, 3, 24], "int32"),
+    "vt": ("sbuf", [128, 2, 2, 24], "float32"),
+    "dd": ("sbuf", [128, 2, 24], "float32"),
+    "cc": ("sbuf", [128, 2, 24], "float32"),
+    "eq": ("sbuf", [128, 24], "float32"),
+    "qq": ("sbuf", [128, 2, 24], "float32"),
+    "mb": ("sbuf", [128, 2, 24], "float32"),
+    "mc": ("sbuf", [128, 24], "float32"),
+    "mx": ("sbuf", [128, 24], "float32"),
+    "offl": ("sbuf", [128, 24], "uint16"),
+    "offr": ("sbuf", [128, 24], "uint16"),
+    "offm": ("sbuf", [128, 24], "uint16"),
+    "ga": ("sbuf", [128, 12 * SL], "bfloat16"),
+    "gb": ("sbuf", [128, 12 * SL], "bfloat16"),
+    "t": ("sbuf", [128, 4 * SL], "bfloat16"),
+    "tq": ("sbuf", [128, 192], "float8_e4m3fn_x4"),
+    "tc": ("sbuf", [128, 192], "uint8"),
+    "tq1": ("sbuf", [128, 128], "float8_e4m3fn_x4"),
+    "tc1": ("sbuf", [128, 128], "uint8"),
+    "tq2": ("sbuf", [128, 128], "float8_e4m3fn_x4"),
+    "tc2": ("sbuf", [128, 128], "uint8"),
+    "rq": ("sbuf", [128, 288], "float8_e4m3fn_x4"),
+    "rc": ("sbuf", [128, 288], "uint8"),
+    "pidx": ("sbuf", [128, 1], "int32"),
+    "pid16": ("sbuf", [128, 1], "int32"),
+    "pp": ("sbuf", [128, 32], "int32"),
+    "pw": ("sbuf", [128, 32], "float32"),
+    "pn": ("sbuf", [128, 16], "float32"),
+    "offf": ("sbuf", [128, 16], "uint16"),
+    "offg": ("sbuf", [128, 16], "uint16"),
+    "zvs": ("sbuf", [128, SL], "float32"),
+    "zus": ("sbuf", [128, SL + 8], "float32"),
+    "y1": ("sbuf", [128, P], "float32"),
+    "ys": ("sbuf", [128, P], "float32"),
+}
+SEMAPHORES = ["sv", "st", "sa", "sg", "dlo", "dln", "dx0", "dx1", "da0", "da1", "da2", "du", "dv", "dy",
+              "gi", "arre", "arrl", "loc"]
+
+
+def rank_program(g, core, T, topo):
+    q = T.rank_of(core)
+    if q is None:
+        return
+    v, ten, act, sy, s = g.vector, g.tensor, g.scalar, g.sync, T.sem
+    cnt = {"sv": 0, "st": 0, "sa": 0, "sg": 0}
+    seen = {}
+
+    def done(ins, name):
+        cnt[name] += 1
+        ins.then_inc(s[name], 1)
+        return (name, cnt[name])
+
+    def need(eng, en, *evs):
+        for name, val in evs:
+            if seen.get((en, name), 0) < val:
+                eng.wait_ge(s[name], val)
+                seen[(en, name)] = val
+
+    def V(ins):
+        return done(ins, "sv")
+
+    def S(ins):
+        return done(ins, "sa")
+
+    def vw(*evs):
+        need(v, "v", *evs)
+
+    sy.dma_start(T.lob[:], T.lo[:]).then_inc(s.dlo, 16)
+    act.dma_start(T.lnb[:], T.ln[:]).then_inc(s.dln, 16)
+    sy.dma_start(T.xs[:, 0:1024], T.x[:, 0:1024]).then_inc(s.dx0, 16)
+    act.dma_start(T.ab[:, 0:512], T.a[:, 0:512]).then_inc(s.da0, 16)
+    sy.dma_start(T.xs[:, 1024:2048], T.x[:, 1024:2048]).then_inc(s.dx1, 16)
+    act.dma_start(T.ab[:, 512:1024], T.a[:, 512:1024]).then_inc(s.da1, 16)
+    sy.dma_start(T.ab[:, 1024:2048], T.a[:, 1024:2048]).then_inc(s.da2, 16)
+    act.dma_start(T.uv[:, 0:512], T.u[:]).then_inc(s.du, 16)
+    sy.dma_start(T.uv[:, 512:1024], T.v[:]).then_inc(s.dv, 16)
+
+    e_iota = done(g.iota(T.pidx[:], [[0, 1]], 0, 1), "sg")
+    done(g.iota(T.mi[:], [[0, SL], [1, 2]], 0, 0, allow_small_or_imprecise_dtypes=True), "sg")
+    e = done(g.iota(T.one[:], [[0, 3 * SL]], 1, 0, allow_small_or_imprecise_dtypes=True), "sg")
+    need(g, "g", e)
+    e_mi = done(g.affine_select(T.m3[:], T.one[:], [[0, SL], [1, 3]], A.not_equal, 0.0, 0, 0), "sg")
+
+    V(v.memset(T.mk[:], 1.0))
+    e = V(v.memset(T.mz[:], 1.0))
+    for p in (0, 1):
+        V(v.memset(T.bt[:, NR * RW * p:NR * RW * p + RW], 0.0))
+    e3 = V(v.memset(T.zus[:, SL:SL + 8], 0.0))
+    vw(e)
+    for n, k in enumerate(LV):
+        V(v.memset(T.mk[:, X * n:X * n + X:1 << k], 0.0))
+    V(v.memset(T.mz[:, NB:2 * NB + 1:NB], 0.0))
+    e_mk = V(v.memset(T.mz[:, 3 * NB + 1:4 * NB + 2:NB], 0.0))
+    vw(e_iota)
+    e_pid = V(v.tensor_scalar(T.pid16[:], T.pidx[:], 15, None, A.bitwise_and))
+    need(g, "g", e_pid)
+    for n, tab in enumerate((T.pf, T.pg)):
+        g.indirect_dma_start(T.pp[:, 16 * n:16 * n + 16], None, tab[:], IndirectOffsetOnAxis(ap=T.pid16[:, 0:1], axis=0),
+                             bounds_check=15).then_inc(s.gi, 16)
+
+    vw(("dlo", 16), ("dln", 16))
+    m = 6 * ((q + 1) % N)
+    runs = [(0, m, 24)] + ([(24 - m, 0, m)] if m else [])
+    for d, a, b in runs:
+        V(v.tensor_copy(T.wt[:, 1, 0, 0, d:d + b - a], T.lob[:, a:b]))
+        e = V(v.tensor_tensor(T.wt[:, 0, 0, 0, d:d + b - a], T.lnb[:, a:b], T.lob[:, a:b], A.add))
+    vw(e)
+    V(v.tensor_scalar(T.wt[:, 1, 1, 0], T.wt[:, 1, 0, 0], -1, None, A.add))
+    e = V(v.tensor_scalar(T.wt[:, 0, 1, 0], T.wt[:, 0, 0, 0], -1, None, A.add))
+    V(v.tensor_scalar(T.cc[:, 0], T.wt[:, 1, 0, 0], 0.5 / X, None, A.mult))
+    vw(e)
+    for n, k in enumerate(LV):
+        e = V(v.tensor_scalar(T.wt[:, :, :, n + 1], T.wt[:, :, :, 0], k, None, A.arith_shift_right))
+    V(v.tensor_scalar(T.cc[:, 1], T.wt[:, 0, 1, 0], -0.5 / X, -float(H0), A.mult, A.add))
+    vw(e)
+    V(v.tensor_tensor(T.vt[:], T.wt[:, 0, :, 1:3], T.wt[:, 1, :, 1:3], A.is_gt))
+    e_dd = V(v.tensor_tensor(T.dd[:], T.wt[:, 0, 1, 1:3], T.wt[:, 1, 0, 1:3], A.subtract))
+    vw(e_dd)
+
+    def ends():
+        for n in (0, 1):
+            e = V(v.tensor_tensor(T.cc[:], T.cc[:], T.vt[:, :, n], A.add))
+            vw(e)
+        V(v.tensor_scalar(T.offl[:], T.cc[:, 0], 2.0 * X, None, A.mult))
+        V(v.tensor_scalar(T.offr[:], T.cc[:, 1], -2.0 * X, None, A.mult))
+
+    def middle_a():
+        V(v.tensor_scalar(T.qq[:], T.dd[:], 2.0, None, A.is_ge))
+        V(v.tensor_scalar(T.eq[:], T.dd[:, 1], 0.0, None, A.is_equal))
+        V(v.tensor_scalar(T.mx[:], T.dd[:, 0], 3.0, float(RW), A.is_ge, A.mult))
+        V(v.tensor_scalar(T.mb[:, 0], T.wt[:, 0, 1, 1], float(RW), float(RW * (CROW - 2)), A.mult, A.add))
+        V(v.tensor_scalar(T.mb[:, 1], T.wt[:, 1, 0, 2], float(RW), float(RW - 1), A.mult, A.add))
+        return V(v.tensor_scalar(T.mc[:], T.wt[:, 0, 1, 2], float(1 - 4 * RW), None, A.mult))
+
+    def middle_b(e):
+        vw(e)
+        V(v.tensor_tensor(T.qq[:, 0], T.qq[:, 0], T.eq[:], A.mult))
+        V(v.tensor_tensor(T.mb[:, 1], T.mb[:, 1], T.wt[:, 0, 1, 2], A.add))
+        e = V(v.tensor_tensor(T.mx[:], T.mx[:], T.mc[:], A.add))
+        vw(e)
+        e = V(v.tensor_tensor(T.mb[:, 0], T.mb[:, 0], T.mx[:], A.add))
+        vw(e)
+        e = V(v.tensor_tensor(T.mb[:], T.mb[:], T.qq[:], A.mult))
+        vw(e)
+        e = V(v.tensor_tensor(T.mx[:], T.mb[:, 0], T.mb[:, 1], A.add))
+        vw(e)
+        return V(v.tensor_copy(T.offm[:], T.mx[:]))
+
+    def quant(dst, sc, src):
+        return V(v.quantize_mx(dst, sc, src))
+
+    def mm(bank, n, w, wc, x, xc):
+        return done(ten.matmul_mx(T.ps[:, 512 * bank:512 * bank + n], w, wc, x, xc, True, True), "st")
+
+    def place(i, t):
+        return X * (2 * (NT * (i // 2) + t) + i % 2)
+
+    def col(i, t, a=0, b=X, st=1):
+        o = place(i, t)
+        return T.tw[:, o + a:o + b:st]
+
+    def back(i, t, a, b):
+        o = place(i, t)
+        return T.tw[:, o + b - 1:(o + a - 1 if o + a else None):-1]
+
+    def relu(i, a, b, bank):
+        return S(act.activation(col(i, H0, a, b), T.ps[:, 512 * bank:512 * bank + b - a], F.Relu, scale=0.05))
+
+    def prod_z(i, c0, c1, bank):
+        return mm(bank, c1 - c0, T.aq[:, 128 * i:128 * i + 128], T.ac[:, 128 * i:128 * i + 128], T.xq[:, c0:c1], T.xc[:, c0:c1])
+
+    vw(("da0", 16))
+    quant(T.aq[:, 0:128], T.ac[:, 0:128], T.ab[:, 0:512])
+    vw(("dx0", 16))
+    e = quant(T.xq[:, 0:256], T.xc[:, 0:256], T.xs[:, 0:1024])
+    need(ten, "t", e)
+    z = prod_z(0, 0, 256, 0)
+    need(act, "a", z)
+    eh0 = relu(0, 0, 256, 0)
+    ends()
+    em = middle_a()
+    ev = {}
+
+    def quant_a(i0, i1, sem):
+        vw((sem, 16))
+        e = quant(T.aq[:, 128 * i0:128 * i1], T.ac[:, 128 * i0:128 * i1], T.ab[:, 512 * i0:512 * i1])
+        need(ten, "t", e)
+        for i in range(i0, i1):
+            z = prod_z(i, 0, 512, i + 1)
+            need(act, "a", z)
+            ev[i] = relu(i, 0, 512, i + 1)
+
+    def scan_s(i, n, a=0, b=X):
+        return V(v.tensor_tensor_scan(back(i, ST[n], a, b), T.mk[:, X * n:X * n + b - a], back(i, H0, a, b), 0.0, A.mult, A.max))
+
+    def scan_p(i, n, a=0, b=X):
+        return V(v.tensor_tensor_scan(col(i, PT[n], a, b), T.mk[:, X * n:X * n + b - a], col(i, H0, a, b), 0.0, A.mult, A.max))
+
+    def middles(p, e):
+        i, o, b = 2 * p, NR * RW * p, 2 * RW * p
+        vw(e)
+        for c in (0, RW):
+            e = V(v.tensor_copy(T.bm[:, b + c:b + c + RW], col(i, P16, 15, 2 * X, 16)))
+        u, w = col(i, P4, 7, 2 * X, 16), col(i, P4, 11, 2 * X, 16)
+        at = o + RW * CROW
+        V(v.tensor_copy(T.bt[:, at:at + RW], u))
+        V(v.tensor_copy(T.bt[:, at + RW:at + 2 * RW], w))
+        V(v.tensor_tensor(T.bt[:, at + 2 * RW:at + 3 * RW], u, w, A.max))
+        vw(e)
+        for r in range(1, NB - 1, 2):
+            e = V(v.tensor_tensor_scan(T.bt[:, o + RW * r:o + RW * (r + 2)], T.mz[:, NB - r:5 * NB - r], T.bm[:, b:b + 2 * RW],
+                                       0.0, A.mult, A.max))
+        return e
+
+    def win(i, n):
+        if n == MID:
+            o = NR * RW * (i // 2)
+            return T.bt[:, o + NB * (i % 2):o + NR * RW]
+        a, b = (H0, S16) if n == LEFT else (P16, H0)
+        return T.tw[:, place(i, a):place(i, b) + X]
+
+    def off(n, c0, c1):
+        return (T.offl, T.offm, T.offr)[n][:, c0 // 16:c1 // 16]
+
+    def gather(i, c0, c1, after, ns, w):
+        o = 3 * SL * i
+        for at, n in ns:
+            need(act, "a", after, e_off)
+            e = S(act.activation(T.ga[:, o + w * c0 + at:o + w * c1:w], win(i, n).indirect(off(n, c0, c1)), F.Copy))
+        return e
+
+    def largest(i, c0, c1, w, e):
+        vw(e, e_mi)
+        o = 3 * SL * i
+        return V(v.tensor_tensor_scan(T.gb[:, o + w * c0:o + w * c1], (T.mi if w == 2 else T.m3)[:, w * c0:w * c1],
+                                      T.ga[:, o + w * c0:o + w * c1], 0.0, A.mult, A.max))
+
+    def last(i, c0, c1, w):
+        o = 3 * SL * i
+        return T.gb[:, o + w * c0 + w - 1:o + w * c1:w]
+
+    def piece(i, c0, c1):
+        return T.t[:, 4 * c0 + i:4 * c1:4]
+
+    def take(i, c0, c1, w, e):
+        vw(e)
+        return V(v.tensor_copy(piece(i, c0, c1), last(i, c0, c1, w)))
+
+    def join(i, c0, c1, w, n, e):
+        vw(e, e_off)
+        return V(v.tensor_tensor(piece(i, c0, c1), win(i, n).indirect(off(n, c0, c1)), last(i, c0, c1, w), A.max))
+
+    vw(e_mk, eh0)
+    for n in (0, 1):
+        scan_p(0, n, 0, 256)
+        scan_s(0, n, 0, 256)
+    vw(("dx1", 16))
+    e = quant(T.xq[:, 256:512], T.xc[:, 256:512], T.xs[:, 1024:2048])
+    need(ten, "t", e)
+    z = prod_z(0, 256, 512, 1)
+    need(act, "a", z)
+    ev[0] = relu(0, 256, 512, 1)
+    quant_a(1, 2, "da1")
+    e_off = middle_b(em)
+    vw(ev[0])
+    for n in (0, 1):
+        scan_s(0, n, 256, X)
+        scan_p(0, n, 256, X)
+    vw(ev[1])
+    scan_s(1, 0)
+    e = scan_s(1, 1)
+    gather(0, *ALL, e, ((0, LEFT),), 3)
+    quant_a(2, 4, "da2")
+    gather(1, *ALL, e, ((0, LEFT),), 2)
+    scan_p(1, 0)
+    e = scan_p(1, 1)
+    gather(0, *ALL, e, ((2, RIGHT),), 3)
+    e = middles(0, e)
+    ga0 = gather(0, *ALL, e, ((1, MID),), 3)
+    ga1 = gather(1, *ALL, e, ((1, MID),), 2)
+    vw(ev[2])
+    for n in (0, 1):
+        scan_s(2, n)
+        scan_p(2, n)
+    vw(ev[3])
+    for n in (0, 1):
+        e = scan_s(3, n)
+    gather(2, *EARLY, e, ((0, LEFT),), 2)
+    gather(3, *EARLY, e, ((0, LEFT),), 2)
+    for n in (0, 1):
+        e = scan_p(3, n)
+    g2 = [gather(2, *EARLY, e, ((1, RIGHT),), 2)]
+    g3 = [gather(3, *EARLY, e, ((1, RIGHT),), 2)]
+    middles(1, e)
+    take(0, *ALL, 3, largest(0, *ALL, 3, ga0))
+    for i, gl in ((2, g2), (3, g3)):
+        gl += 2 * [gather(i, *REST, e, ((0, LEFT), (1, RIGHT)), 2)]
+    join(1, *ALL, 2, RIGHT, largest(1, *ALL, 2, ga1))
+
+    def pieces(n):
+        c = CUTS[n]
+        a = largest(2, *c, 2, g2[n])
+        b = largest(3, *c, 2, g3[n])
+        join(2, *c, 2, MID, a)
+        vw(join(3, *c, 2, MID, b))
+
+    def dst(r):
+        rid, pnc, _ = topo.addr(T.cores[r])
+        return DstId(rid=rid, pnc=pnc)
+
+    def send(js, sq, sc, c0, sem):
+        for kind in (0, 1):
+            tr = []
+            for n, j in enumerate(js):
+                r = (q + 1 + j) % N
+                eng = topo.engines(core, T.cores[r])
+                w = len(eng) // len(js)
+                m = sum(1 << x for x in eng[n * w:n * w + w])
+                a, b, at = c0 + n * CAPP, c0 + (n + 1) * CAPP, CAPP * (2 - j)
+                if kind == 0:
+                    sa, da = sq[:, a:b].bitcast(dt.uint8), T.rq[:, at:at + CAPP].bitcast(dt.uint8)
+                else:
+                    sa, da = sc[:, a:b], T.rc[:, at:at + CAPP]
+                tr.append(RemoteDMATransfer(dst_ids=[dst(r)], dma_engine_mask=m, remote_sem=sem, src=sa, dst=da))
+            g.remote_dma_fused(tr, local_sem=s.loc)
+
+    pieces(0)
+    e = quant(T.tq[:], T.tc[:], T.t[:, 0:768])
+    need(g, "g", e)
+    send([0, 1], T.tq, T.tc, 0, s.arre)
+    pieces(1)
+    e = quant(T.tq1[:], T.tc1[:], T.t[:, 640:1152])
+    need(g, "g", e)
+    send([2], T.tq1, T.tc1, 32, s.arrl)
+    pieces(2)
+    e_own = quant(T.tq2[:], T.tc2[:], T.t[:, 1024:1536])
+    vw(("du", 16), ("dv", 16))
+    e_uv = quant(T.uvq[:], T.uvc[:], T.uv[:])
+
+    c1 = CAPP * (q + 1)
+    vw(("gi", 32))
+    V(v.tensor_scalar(T.pn[:], T.pp[:, 16:32], 0, 1 + c1, A.is_lt, A.mult))
+    e = V(v.tensor_scalar(T.pw[:], T.pp[:], c1, SL, A.is_lt, A.mult))
+    vw(e)
+    e = V(v.tensor_tensor(T.pw[:], T.pw[:], T.pp[:], A.add))
+    vw(e)
+    e_f = V(v.tensor_scalar(T.offf[:], T.pw[:, 0:16], -c1, None, A.add))
+    e = V(v.tensor_tensor(T.pn[:], T.pn[:], T.pw[:, 16:32], A.add))
+    vw(e)
+    e_g = V(v.tensor_scalar(T.offg[:], T.pn[:], -c1, None, A.add))
+
+    def prod(x, xc, n, skip, m, at, bv, bu):
+        ev_ = mm(bv, n, T.uvq[:, 128:256], T.uvc[:, 128:256], x, xc)
+        eu = mm(bu, n, T.uvq[:, 0:128], T.uvc[:, 0:128], x, xc)
+        need(act, "a", ev_)
+        a = S(act.activation(T.zvs[:, at:at + m], T.ps[:, 512 * bv + skip:512 * bv + skip + m], F.Copy))
+        vw(eu)
+        b = V(v.tensor_copy(T.zus[:, at:at + m], T.ps[:, 512 * bu + skip:512 * bu + skip + m]))
+        return a, b
+
+    need(ten, "t", e_own, e_uv)
+    prod(T.tq2[:], T.tc2[:], 128, 32, CAPP, 288, 5, 6)
+    need(ten, "t", ("arre", 16), ev[3])
+    prod(T.rq[:, 96:288], T.rc[:, 96:288], 192, 0, 192, 96, 7, 0)
+    need(ten, "t", ("arrl", 16))
+    a, b = prod(T.rq[:, 0:128], T.rc[:, 0:128], 128, 0, CAPP, 0, 1, 2)
+    H = 96
+    need(act, "a", a, e_f)
+    e = S(act.activation(T.y1[:, H:P], T.zvs[:].indirect(T.offf[:, H // 16:P // 16]), F.Copy))
+    vw(a, b, e_g, e3)
+    vw(V(v.tensor_copy(T.y1[:, 0:H], T.zvs[:].indirect(T.offf[:, 0:H // 16]))))
+    for c, d in ((0, H), (H, P)):
+        if c:
+            vw(e)
+        o = V(v.tensor_tensor(T.ys[:, c:d], T.zus[:].indirect(T.offg[:, c // 16:d // 16]), T.y1[:, c:d], A.add))
+        need(sy, "s", o)
+        sy.dma_start(T.y[:, c:d], T.ys[:, c:d]).then_inc(s.dy, 16)
+    sy.wait_ge(s.dy, 32)
+    g.wait_ge(s.loc, 32)
+    for name in ("sv", "st", "sa", "sg"):
+        need(g, "g", (name, cnt[name]))

@@ -8,17 +8,21 @@ CAPP = 96
 P = 256
 SL = N * CAPP
 X = 512
-LV = (2, 4)
-P16, P4, H0, S4, S16, NT = 0, 1, 2, 3, 4, 5
-PT = (P4, P16)
-ST = (S4, S16)
-NB = X // 16
-RW = 2 * NB
-NR = 35
-CROW = 32
+HALF = X // 2
+SH = (1, 3, 6)
+BL = (8, 64)
+P64, P8, H0, S8, S64, NT = 0, 1, 2, 3, 4, 5
+PT = (P8, P64)
+ST = (S8, S64)
+BIG = 1e29
+NG = X // 8 + 8
+SEC = 8 * NG
+C0 = 1041
+Z0 = C0 - X - 1
+B12 = 1616
+PAIR = B12 + 2 * SEC
 LEFT, MID, RIGHT = 0, 1, 2
-CUTS = ((0, 2 * CAPP), (2 * CAPP, 3 * CAPP), (3 * CAPP, SL))
-ALL, EARLY, REST = (0, SL), CUTS[0], (2 * CAPP, SL)
+REM = 3 * CAPP
 
 SCRATCH = {
     "xs": ("sbuf", [128, 2048], "bfloat16"),
@@ -32,42 +36,30 @@ SCRATCH = {
     "uvc": ("sbuf", [128, 256], "uint8"),
     "ps": ("psum", [128, 4096], "float32"),
     "tw": ("sbuf", [128, 4 * NT * X], "bfloat16"),
-    "bm": ("sbuf", [128, 4 * RW], "bfloat16"),
-    "bt": ("sbuf", [128, 2 * NR * RW], "bfloat16"),
-    "mk": ("sbuf", [128, 2 * X], "bfloat16"),
-    "mz": ("sbuf", [128, 5 * NB], "bfloat16"),
-    "mi": ("sbuf", [128, 2 * SL], "bfloat16"),
-    "one": ("sbuf", [128, 3 * SL], "bfloat16"),
-    "m3": ("sbuf", [128, 3 * SL], "bfloat16"),
+    "bm": ("sbuf", [128, 4 * NG], "bfloat16"),
+    "bt": ("sbuf", [128, 2 * PAIR], "bfloat16"),
+    "cp": ("sbuf", [128, 2 * X + 72], "bfloat16"),
+    "cr": ("sbuf", [128, 14 * NG], "bfloat16"),
+    "mi": ("sbuf", [128, 2 * CAPP], "bfloat16"),
+    "m3": ("sbuf", [128, 3 * CAPP], "bfloat16"),
     "lnb": ("sbuf", [128, 24], "int32"),
-    "lob": ("sbuf", [128, 24], "int32"),
-    "wt": ("sbuf", [128, 2, 2, 3, 24], "int32"),
-    "vt": ("sbuf", [128, 2, 2, 24], "float32"),
-    "dd": ("sbuf", [128, 2, 24], "float32"),
-    "cc": ("sbuf", [128, 2, 24], "float32"),
-    "eq": ("sbuf", [128, 24], "float32"),
-    "qq": ("sbuf", [128, 2, 24], "float32"),
-    "mb": ("sbuf", [128, 2, 24], "float32"),
-    "mc": ("sbuf", [128, 24], "float32"),
-    "mx": ("sbuf", [128, 24], "float32"),
-    "offl": ("sbuf", [128, 24], "uint16"),
-    "offr": ("sbuf", [128, 24], "uint16"),
-    "offm": ("sbuf", [128, 24], "uint16"),
+    "xt": ("sbuf", [128, 2, 24], "int32"),
+    "tt": ("sbuf", [128, 3, 2, 24], "int32"),
+    "gg": ("sbuf", [128, 2, 24], "float32"),
+    "gs": ("sbuf", [128, 24], "float32"),
+    "mm": ("sbuf", [128, 3, 24], "float32"),
+    "oo": ("sbuf", [128, 3, 24], "float32"),
+    "off": ("sbuf", [128, 3, 24], "uint16"),
     "ga": ("sbuf", [128, 12 * SL], "bfloat16"),
     "gb": ("sbuf", [128, 12 * SL], "bfloat16"),
-    "t": ("sbuf", [128, 4 * SL], "bfloat16"),
-    "tq": ("sbuf", [128, 192], "float8_e4m3fn_x4"),
-    "tc": ("sbuf", [128, 192], "uint8"),
-    "tq1": ("sbuf", [128, 128], "float8_e4m3fn_x4"),
-    "tc1": ("sbuf", [128, 128], "uint8"),
-    "tq2": ("sbuf", [128, 128], "float8_e4m3fn_x4"),
-    "tc2": ("sbuf", [128, 128], "uint8"),
-    "rq": ("sbuf", [128, 288], "float8_e4m3fn_x4"),
-    "rc": ("sbuf", [128, 288], "uint8"),
+    "t": ("sbuf", [128, N, 512], "bfloat16"),
+    "tq": ("sbuf", [128, 512], "float8_e4m3fn_x4"),
+    "tc": ("sbuf", [128, 512], "uint8"),
+    "rq": ("sbuf", [128, REM], "float8_e4m3fn_x4"),
+    "rc": ("sbuf", [128, REM], "uint8"),
     "pidx": ("sbuf", [128, 1], "int32"),
     "pid16": ("sbuf", [128, 1], "int32"),
     "pp": ("sbuf", [128, 32], "int32"),
-    "pw": ("sbuf", [128, 32], "float32"),
     "pn": ("sbuf", [128, 16], "float32"),
     "offf": ("sbuf", [128, 16], "uint16"),
     "offg": ("sbuf", [128, 16], "uint16"),
@@ -105,89 +97,88 @@ def rank_program(g, core, T, topo):
     def S(ins):
         return done(ins, "sa")
 
+    def G(ins):
+        return done(ins, "sg")
+
     def vw(*evs):
         need(v, "v", *evs)
 
-    sy.dma_start(T.lob[:], T.lo[:]).then_inc(s.dlo, 16)
+    def aw(*evs):
+        need(act, "a", *evs)
+
+    def order(r):
+        far = [(r + 1 + j) % N for j in range(N - 1)]
+        return sorted(far, key=lambda k: topo.same_plane(topo.chip(T.cores[r]), topo.chip(T.cores[k])))
+
+    sy.dma_start(T.xt[:, 0], T.lo[:]).then_inc(s.dlo, 16)
     act.dma_start(T.lnb[:], T.ln[:]).then_inc(s.dln, 16)
-    sy.dma_start(T.xs[:, 0:1024], T.x[:, 0:1024]).then_inc(s.dx0, 16)
     act.dma_start(T.ab[:, 0:512], T.a[:, 0:512]).then_inc(s.da0, 16)
-    sy.dma_start(T.xs[:, 1024:2048], T.x[:, 1024:2048]).then_inc(s.dx1, 16)
+    sy.dma_start(T.xs[:, 0:1024], T.x[:, 0:1024]).then_inc(s.dx0, 16)
     act.dma_start(T.ab[:, 512:1024], T.a[:, 512:1024]).then_inc(s.da1, 16)
+    sy.dma_start(T.xs[:, 1024:2048], T.x[:, 1024:2048]).then_inc(s.dx1, 16)
     sy.dma_start(T.ab[:, 1024:2048], T.a[:, 1024:2048]).then_inc(s.da2, 16)
-    act.dma_start(T.uv[:, 0:512], T.u[:]).then_inc(s.du, 16)
+    sy.dma_start(T.uv[:, 0:512], T.u[:]).then_inc(s.du, 16)
     sy.dma_start(T.uv[:, 512:1024], T.v[:]).then_inc(s.dv, 16)
 
-    e_iota = done(g.iota(T.pidx[:], [[0, 1]], 0, 1), "sg")
-    done(g.iota(T.mi[:], [[0, SL], [1, 2]], 0, 0, allow_small_or_imprecise_dtypes=True), "sg")
-    e = done(g.iota(T.one[:], [[0, 3 * SL]], 1, 0, allow_small_or_imprecise_dtypes=True), "sg")
-    need(g, "g", e)
-    e_mi = done(g.affine_select(T.m3[:], T.one[:], [[0, SL], [1, 3]], A.not_equal, 0.0, 0, 0), "sg")
-
-    V(v.memset(T.mk[:], 1.0))
-    e = V(v.memset(T.mz[:], 1.0))
-    for p in (0, 1):
-        V(v.memset(T.bt[:, NR * RW * p:NR * RW * p + RW], 0.0))
-    e3 = V(v.memset(T.zus[:, SL:SL + 8], 0.0))
-    vw(e)
-    for n, k in enumerate(LV):
-        V(v.memset(T.mk[:, X * n:X * n + X:1 << k], 0.0))
-    V(v.memset(T.mz[:, NB:2 * NB + 1:NB], 0.0))
-    e_mk = V(v.memset(T.mz[:, 3 * NB + 1:4 * NB + 2:NB], 0.0))
+    e_iota = G(g.iota(T.pidx[:], [[0, 1]], 0, 1))
+    CP = (0, X + 8)
+    e = V(v.memset(T.cp[:], BIG))
+    e_big = V(v.memset(T.m3[:], BIG))
+    V(v.memset(T.zus[:, SL:SL + 8], 0.0))
     vw(e_iota)
     e_pid = V(v.tensor_scalar(T.pid16[:], T.pidx[:], 15, None, A.bitwise_and))
+    vw(e_big)
+    V(v.memset(T.m3[:, 0:3 * CAPP:3], 0.0))
+    for n, b in enumerate(BL):
+        e_cp = V(v.memset(T.cp[:, CP[n]:CP[n] + X + b:b], 0.0))
+    aw(e_cp)
+    e_cr = S(act.activation(T.cr[:], T.cp[:, 0:14 * NG], F.Identity, bias=BIG, scale=0.0))
+
+    def zeros(out, n):
+        return S(act.activation(out, T.cp[:, 0:n], F.Copy, scale=0.0))
+
+    def clear(p):
+        o = PAIR * p
+        zeros(T.bt[:, o + Z0:o + B12:2], (B12 - Z0) // 2)
+        return zeros(T.bt[:, o + B12 + 7:o + PAIR:8], 2 * NG)
+
+    e_bz = [clear(0)]
+    G(g.iota(T.mi[:], [[0, CAPP], [1, 2]], 0, 0, allow_small_or_imprecise_dtypes=True))
+    e_t = G(g.iota(T.t[:, :, 4 * CAPP:512], [[0, N], [0, 128]], 0, 0, allow_small_or_imprecise_dtypes=True))
+    need(g, "g", e_cr)
+    e_cr = G(g.affine_select(T.cr[:], T.cr[:], [[-1, 7], [0, NG // 4], [1, 8]], A.is_gt, 0.0, 0, 0))
     need(g, "g", e_pid)
     for n, tab in enumerate((T.pf, T.pg)):
         g.indirect_dma_start(T.pp[:, 16 * n:16 * n + 16], None, tab[:], IndirectOffsetOnAxis(ap=T.pid16[:, 0:1], axis=0),
                              bounds_check=15).then_inc(s.gi, 16)
 
-    vw(("dlo", 16), ("dln", 16))
     m = 6 * ((q + 1) % N)
     runs = [(0, m, 24)] + ([(24 - m, 0, m)] if m else [])
-    for d, a, b in runs:
-        V(v.tensor_copy(T.wt[:, 1, 0, 0, d:d + b - a], T.lob[:, a:b]))
-        e = V(v.tensor_tensor(T.wt[:, 0, 0, 0, d:d + b - a], T.lnb[:, a:b], T.lob[:, a:b], A.add))
-    vw(e)
-    V(v.tensor_scalar(T.wt[:, 1, 1, 0], T.wt[:, 1, 0, 0], -1, None, A.add))
-    e = V(v.tensor_scalar(T.wt[:, 0, 1, 0], T.wt[:, 0, 0, 0], -1, None, A.add))
-    V(v.tensor_scalar(T.cc[:, 0], T.wt[:, 1, 0, 0], 0.5 / X, None, A.mult))
-    vw(e)
-    for n, k in enumerate(LV):
-        e = V(v.tensor_scalar(T.wt[:, :, :, n + 1], T.wt[:, :, :, 0], k, None, A.arith_shift_right))
-    V(v.tensor_scalar(T.cc[:, 1], T.wt[:, 0, 1, 0], -0.5 / X, -float(H0), A.mult, A.add))
-    vw(e)
-    V(v.tensor_tensor(T.vt[:], T.wt[:, 0, :, 1:3], T.wt[:, 1, :, 1:3], A.is_gt))
-    e_dd = V(v.tensor_tensor(T.dd[:], T.wt[:, 0, 1, 1:3], T.wt[:, 1, 0, 1:3], A.subtract))
-    vw(e_dd)
+    ts, tt = v.tensor_scalar, v.tensor_tensor
+    base = (C0, B12 - 8, B12 - 8 + 8 * (X // 8))
+    steps = [
+        [lambda: tt(T.xt[:, 1], T.xt[:, 0], T.lnb[:], A.add)],
+        [lambda: ts(T.xt[:, 1], T.xt[:, 1], 1, None, A.add)],
+        [lambda k=k: ts(T.tt[:, k], T.xt[:], SH[k], None, A.arith_shift_right) for k in (1, 2, 0)],
+        [lambda: tt(T.gg[:], T.tt[:, 1:3, 1], T.tt[:, 1:3, 0], A.is_gt)]
+        + [lambda k=k: ts(T.mm[:, k], T.tt[:, k, 1], (-3.0, 8.0, 8.0)[k], float(base[k] - X + 1), A.mult, A.add) for k in range(3)],
+        [lambda: tt(T.gs[:], T.gg[:, 0], T.gg[:, 1], A.add), lambda: ts(T.tt[:, 1, 0], T.tt[:, 1, 0], 7, None, A.bitwise_and)],
+        [lambda: ts(T.gs[:], T.gs[:], float(X), float(1 - X), A.mult, A.add), lambda: tt(T.mm[:], T.mm[:], T.tt[:, :, 0], A.add)],
+        [lambda: tt(T.mm[:, 1:3], T.mm[:, 1:3], T.gg[:], A.mult), lambda: tt(T.oo[:, LEFT], T.xt[:, 0], T.gs[:], A.add),
+         lambda: tt(T.oo[:, RIGHT], T.xt[:, 1], T.gs[:], A.subtract)],
+        [lambda: tt(T.mm[:, 1], T.mm[:, 1], T.mm[:, 2], A.max)],
+        [lambda: tt(T.oo[:, MID], T.mm[:, 0], T.mm[:, 1], A.max)],
+        [lambda d=d, a=a, b=b: ts(T.off[:, :, d:d + b - a], T.oo[:, :, a:b], float(X - 1), None, A.add) for d, a, b in runs],
+    ]
+    at = {"step": 0, "e": [("dlo", 16), ("dln", 16)]}
 
-    def ends():
-        for n in (0, 1):
-            e = V(v.tensor_tensor(T.cc[:], T.cc[:], T.vt[:, :, n], A.add))
-            vw(e)
-        V(v.tensor_scalar(T.offl[:], T.cc[:, 0], 2.0 * X, None, A.mult))
-        V(v.tensor_scalar(T.offr[:], T.cc[:, 1], -2.0 * X, None, A.mult))
-
-    def middle_a():
-        V(v.tensor_scalar(T.qq[:], T.dd[:], 2.0, None, A.is_ge))
-        V(v.tensor_scalar(T.eq[:], T.dd[:, 1], 0.0, None, A.is_equal))
-        V(v.tensor_scalar(T.mx[:], T.dd[:, 0], 3.0, float(RW), A.is_ge, A.mult))
-        V(v.tensor_scalar(T.mb[:, 0], T.wt[:, 0, 1, 1], float(RW), float(RW * (CROW - 2)), A.mult, A.add))
-        V(v.tensor_scalar(T.mb[:, 1], T.wt[:, 1, 0, 2], float(RW), float(RW - 1), A.mult, A.add))
-        return V(v.tensor_scalar(T.mc[:], T.wt[:, 0, 1, 2], float(1 - 4 * RW), None, A.mult))
-
-    def middle_b(e):
-        vw(e)
-        V(v.tensor_tensor(T.qq[:, 0], T.qq[:, 0], T.eq[:], A.mult))
-        V(v.tensor_tensor(T.mb[:, 1], T.mb[:, 1], T.wt[:, 0, 1, 2], A.add))
-        e = V(v.tensor_tensor(T.mx[:], T.mx[:], T.mc[:], A.add))
-        vw(e)
-        e = V(v.tensor_tensor(T.mb[:, 0], T.mb[:, 0], T.mx[:], A.add))
-        vw(e)
-        e = V(v.tensor_tensor(T.mb[:], T.mb[:], T.qq[:], A.mult))
-        vw(e)
-        e = V(v.tensor_tensor(T.mx[:], T.mb[:, 0], T.mb[:, 1], A.add))
-        vw(e)
-        return V(v.tensor_copy(T.offm[:], T.mx[:]))
+    def index(n):
+        for _ in range(n):
+            vw(*at["e"])
+            for call in steps[at["step"]]:
+                at["e"] = [V(call())]
+            at["step"] += 1
+        return at["e"][0]
 
     def quant(dst, sc, src):
         return V(v.quantize_mx(dst, sc, src))
@@ -195,230 +186,211 @@ def rank_program(g, core, T, topo):
     def mm(bank, n, w, wc, x, xc):
         return done(ten.matmul_mx(T.ps[:, 512 * bank:512 * bank + n], w, wc, x, xc, True, True), "st")
 
-    def place(i, t):
-        return X * (2 * (NT * (i // 2) + t) + i % 2)
-
     def col(i, t, a=0, b=X, st=1):
-        o = place(i, t)
+        o = X * (NT * i + t)
         return T.tw[:, o + a:o + b:st]
 
     def back(i, t, a, b):
-        o = place(i, t)
-        return T.tw[:, o + b - 1:(o + a - 1 if o + a else None):-1]
+        o = X * (NT * i + t)
+        return T.tw[:, o + b - 1:o + a - 1:-1]
 
-    def relu(i, a, b, bank):
+    def make_h(i, a, b, bank, e):
+        need(ten, "t", e)
+        z = mm(bank, b - a, T.aq[:, 128 * i:128 * i + 128], T.ac[:, 128 * i:128 * i + 128], T.xq[:, a:b], T.xc[:, a:b])
+        aw(z)
         return S(act.activation(col(i, H0, a, b), T.ps[:, 512 * bank:512 * bank + b - a], F.Relu, scale=0.05))
-
-    def prod_z(i, c0, c1, bank):
-        return mm(bank, c1 - c0, T.aq[:, 128 * i:128 * i + 128], T.ac[:, 128 * i:128 * i + 128], T.xq[:, c0:c1], T.xc[:, c0:c1])
-
-    vw(("da0", 16))
-    quant(T.aq[:, 0:128], T.ac[:, 0:128], T.ab[:, 0:512])
-    vw(("dx0", 16))
-    e = quant(T.xq[:, 0:256], T.xc[:, 0:256], T.xs[:, 0:1024])
-    need(ten, "t", e)
-    z = prod_z(0, 0, 256, 0)
-    need(act, "a", z)
-    eh0 = relu(0, 0, 256, 0)
-    ends()
-    em = middle_a()
-    ev = {}
 
     def quant_a(i0, i1, sem):
         vw((sem, 16))
-        e = quant(T.aq[:, 128 * i0:128 * i1], T.ac[:, 128 * i0:128 * i1], T.ab[:, 512 * i0:512 * i1])
-        need(ten, "t", e)
-        for i in range(i0, i1):
-            z = prod_z(i, 0, 512, i + 1)
-            need(act, "a", z)
-            ev[i] = relu(i, 0, 512, i + 1)
+        return quant(T.aq[:, 128 * i0:128 * i1], T.ac[:, 128 * i0:128 * i1], T.ab[:, 512 * i0:512 * i1])
 
-    def scan_s(i, n, a=0, b=X):
-        return V(v.tensor_tensor_scan(back(i, ST[n], a, b), T.mk[:, X * n:X * n + b - a], back(i, H0, a, b), 0.0, A.mult, A.max))
+    def quant_x(a, b, sem):
+        vw((sem, 16))
+        return quant(T.xq[:, a:b], T.xc[:, a:b], T.xs[:, 4 * a:4 * b])
 
-    def scan_p(i, n, a=0, b=X):
-        return V(v.tensor_tensor_scan(col(i, PT[n], a, b), T.mk[:, X * n:X * n + b - a], col(i, H0, a, b), 0.0, A.mult, A.max))
+    def scan_s(i, a=0, b=X):
+        for n in (0, 1):
+            e = V(v.tensor_tensor_scan(back(i, ST[n], a, b), back(i, H0, a, b), T.cp[:, CP[n]:CP[n] + b - a], 0.0, A.max, A.min))
+        return e
 
-    def middles(p, e):
-        i, o, b = 2 * p, NR * RW * p, 2 * RW * p
+    def scan_p(i, a=0, b=X):
+        for n in (0, 1):
+            first = col(i, PT[n], a - 1, a) if a else 0.0
+            e = V(v.tensor_tensor_scan(col(i, PT[n], a, b), col(i, H0, a, b), T.cp[:, CP[n] + 2:CP[n] + 2 + b - a],
+                                       first, A.max, A.min))
+        return e
+
+    def inner(i, k):
+        o = PAIR * (i // 2) + SEC * (i % 2) + C0 - k
+        return T.bt[:, o:o - X:-8]
+
+    def pairs(i):
+        vw(e_bz[i // 2])
+        V(tt(inner(i, 6), col(i, H0, 1, X, 8), col(i, H0, 2, X, 8), A.max))
+        return V(tt(inner(i, 8), col(i, H0, 3, X, 8), col(i, H0, 4, X, 8), A.max))
+
+    def blocks(i):
+        o = NG * i
+        V(tt(T.bm[:, o:o + 64], col(i, P8, 5, X, 8), col(i, H0, 6, X, 8), A.max))
+        return V(tt(T.bm[:, o + 64:o + NG], col(i, P64, 61, X, 64), col(i, H0, 62, X, 64), A.max))
+
+    def middles(p):
+        i, o = 2 * p, PAIR * p + B12
+        e = pairs(i)
         vw(e)
-        for c in (0, RW):
-            e = V(v.tensor_copy(T.bm[:, b + c:b + c + RW], col(i, P16, 15, 2 * X, 16)))
-        u, w = col(i, P4, 7, 2 * X, 16), col(i, P4, 11, 2 * X, 16)
-        at = o + RW * CROW
-        V(v.tensor_copy(T.bt[:, at:at + RW], u))
-        V(v.tensor_copy(T.bt[:, at + RW:at + 2 * RW], w))
-        V(v.tensor_tensor(T.bt[:, at + 2 * RW:at + 3 * RW], u, w, A.max))
+        blocks(i)
+        e = pairs(i + 1)
+        f = blocks(i + 1)
         vw(e)
-        for r in range(1, NB - 1, 2):
-            e = V(v.tensor_tensor_scan(T.bt[:, o + RW * r:o + RW * (r + 2)], T.mz[:, NB - r:5 * NB - r], T.bm[:, b:b + 2 * RW],
-                                       0.0, A.mult, A.max))
+        for k in (i, i + 1):
+            V(tt(inner(k, 9), inner(k, 6), inner(k, 8), A.max))
+        vw(f, e_cr)
+        for a in range(7):
+            e = V(v.tensor_tensor_scan(T.bt[:, o + a:o + 2 * SEC:8], T.bm[:, 2 * NG * p:2 * NG * (p + 1)],
+                                       T.cr[:, 2 * NG * a:2 * NG * (a + 1)], 0.0, A.max, A.min))
         return e
 
     def win(i, n):
         if n == MID:
-            o = NR * RW * (i // 2)
-            return T.bt[:, o + NB * (i % 2):o + NR * RW]
-        a, b = (H0, S16) if n == LEFT else (P16, H0)
-        return T.tw[:, place(i, a):place(i, b) + X]
+            o = PAIR * (i // 2)
+            return T.bt[:, o + SEC * (i % 2):o + PAIR]
+        o = X * (NT * i + (H0 if n == LEFT else P64))
+        return T.tw[:, o:o + 3 * X]
 
-    def off(n, c0, c1):
-        return (T.offl, T.offm, T.offr)[n][:, c0 // 16:c1 // 16]
+    def off(n, j0, j1):
+        return T.off[:, n, 6 * j0:6 * j1]
 
-    def gather(i, c0, c1, after, ns, w):
+    def gather(i, j0, j1, after, ns, w):
         o = 3 * SL * i
-        for at, n in ns:
-            need(act, "a", after, e_off)
-            e = S(act.activation(T.ga[:, o + w * c0 + at:o + w * c1:w], win(i, n).indirect(off(n, c0, c1)), F.Copy))
+        for k, n in ns:
+            aw(after, e_off)
+            e = S(act.activation(T.ga[:, o + w * CAPP * j0 + k:o + w * CAPP * j1:w], win(i, n).indirect(off(n, j0, j1)), F.Copy))
         return e
 
-    def largest(i, c0, c1, w, e):
-        vw(e, e_mi)
-        o = 3 * SL * i
-        return V(v.tensor_tensor_scan(T.gb[:, o + w * c0:o + w * c1], (T.mi if w == 2 else T.m3)[:, w * c0:w * c1],
-                                      T.ga[:, o + w * c0:o + w * c1], 0.0, A.mult, A.max))
-
-    def last(i, c0, c1, w):
-        o = 3 * SL * i
-        return T.gb[:, o + w * c0 + w - 1:o + w * c1:w]
-
-    def piece(i, c0, c1):
-        return T.t[:, 4 * c0 + i:4 * c1:4]
-
-    def take(i, c0, c1, w, e):
+    def largest(i, j, w, e):
         vw(e)
-        return V(v.tensor_copy(piece(i, c0, c1), last(i, c0, c1, w)))
+        o, n = 3 * SL * i + w * CAPP * j, w * CAPP
+        mask, op = (T.mi, A.mult) if w == 2 else (T.m3, A.min)
+        return V(v.tensor_tensor_scan(T.gb[:, o:o + n], mask[:], T.ga[:, o:o + n], 0.0, op, A.max))
 
-    def join(i, c0, c1, w, n, e):
-        vw(e, e_off)
-        return V(v.tensor_tensor(piece(i, c0, c1), win(i, n).indirect(off(n, c0, c1)), last(i, c0, c1, w), A.max))
+    def finish(i, j, w, e):
+        vw(e)
+        o = 3 * SL * i + w * CAPP * j
+        last, piece = T.gb[:, o + w - 1:o + w * CAPP:w], T.t[:, j, i:4 * CAPP:4]
+        if w == 3:
+            return V(v.tensor_copy(piece, last))
+        return V(tt(piece, win(i, MID).indirect(off(MID, j, j + 1)), last, A.max))
 
-    vw(e_mk, eh0)
-    for n in (0, 1):
-        scan_p(0, n, 0, 256)
-        scan_s(0, n, 0, 256)
-    vw(("dx1", 16))
-    e = quant(T.xq[:, 256:512], T.xc[:, 256:512], T.xs[:, 1024:2048])
-    need(ten, "t", e)
-    z = prod_z(0, 256, 512, 1)
-    need(act, "a", z)
-    ev[0] = relu(0, 256, 512, 1)
-    quant_a(1, 2, "da1")
-    e_off = middle_b(em)
-    vw(ev[0])
-    for n in (0, 1):
-        scan_s(0, n, 256, X)
-        scan_p(0, n, 256, X)
-    vw(ev[1])
-    scan_s(1, 0)
-    e = scan_s(1, 1)
-    gather(0, *ALL, e, ((0, LEFT),), 3)
-    quant_a(2, 4, "da2")
-    gather(1, *ALL, e, ((0, LEFT),), 2)
-    scan_p(1, 0)
-    e = scan_p(1, 1)
-    gather(0, *ALL, e, ((2, RIGHT),), 3)
-    e = middles(0, e)
-    ga0 = gather(0, *ALL, e, ((1, MID),), 3)
-    ga1 = gather(1, *ALL, e, ((1, MID),), 2)
-    vw(ev[2])
-    for n in (0, 1):
-        scan_s(2, n)
-        scan_p(2, n)
-    vw(ev[3])
-    for n in (0, 1):
-        e = scan_s(3, n)
-    gather(2, *EARLY, e, ((0, LEFT),), 2)
-    gather(3, *EARLY, e, ((0, LEFT),), 2)
-    for n in (0, 1):
-        e = scan_p(3, n)
-    g2 = [gather(2, *EARLY, e, ((1, RIGHT),), 2)]
-    g3 = [gather(3, *EARLY, e, ((1, RIGHT),), 2)]
-    middles(1, e)
-    take(0, *ALL, 3, largest(0, *ALL, 3, ga0))
-    for i, gl in ((2, g2), (3, g3)):
-        gl += 2 * [gather(i, *REST, e, ((0, LEFT), (1, RIGHT)), 2)]
-    join(1, *ALL, 2, RIGHT, largest(1, *ALL, 2, ga1))
+    def pieces(j, ws, es):
+        big = [largest(i, j, ws[i], es[i]) for i in range(4)]
+        for i in range(4):
+            e = finish(i, j, ws[i], big[i])
+        vw(e, e_t)
+        return quant(T.tq[:, 128 * j:128 * j + 128], T.tc[:, 128 * j:128 * j + 128], T.t[:, j])
 
-    def pieces(n):
-        c = CUTS[n]
-        a = largest(2, *c, 2, g2[n])
-        b = largest(3, *c, 2, g3[n])
-        join(2, *c, 2, MID, a)
-        vw(join(3, *c, 2, MID, b))
+    cuts = [(r - q - 1) % N for r in order(q)]
+    index(4)
+    quant_a(0, 1, "da0")
+    e = quant_x(0, HALF, "dx0")
+    h00 = make_h(0, 0, HALF, 0, e)
+    h10 = make_h(1, 0, HALF, 1, quant_a(1, 2, "da1"))
+    e_bz.append(clear(1))
+    index(3)
+    vw(e_cp, h00)
+    scan_p(0, 0, HALF)
+    scan_s(0, 0, HALF)
+    e = quant_x(HALF, X, "dx1")
+    h01 = make_h(0, HALF, X, 2, e)
+    h11 = make_h(1, HALF, X, 3, e)
+    index(1)
+    vw(h10)
+    scan_p(1, 0, HALF)
+    index(1)
+    scan_s(1, 0, HALF)
+    e_off = index(1)
+    vw(h01)
+    e = scan_s(0, HALF, X)
+    gather(0, 0, 3, e, ((0, LEFT),), 3)
+    e = scan_p(0, HALF, X)
+    gather(0, 0, 3, e, ((2, RIGHT),), 3)
+    e = quant_a(2, 4, "da2")
+    h2 = make_h(2, 0, X, 4, e)
+    h3 = make_h(3, 0, X, 5, e)
+    vw(h11)
+    e = scan_s(1, HALF, X)
+    gather(1, 0, 3, e, ((0, LEFT),), 3)
+    e = scan_p(1, HALF, X)
+    gather(1, 0, 3, e, ((2, RIGHT),), 3)
+    e = middles(0)
+    g0 = gather(0, 0, 3, e, ((1, MID),), 3)
+    g1 = gather(1, 0, 3, e, ((1, MID),), 3)
+    ends = {}
+    for i, h in ((2, h2), (3, h3)):
+        vw(h)
+        es = scan_s(i)
+        ends[i] = (es, scan_p(i))
+    e_rows = middles(1)
+    got = {}
+    for j in cuts:
+        for i in (2, 3):
+            gather(i, j, j + 1, ends[i][0], ((0, LEFT),), 2)
+            got[i, j] = gather(i, j, j + 1, ends[i][1], ((1, RIGHT),), 2)
+    own = [gather(i, 3, 4, e_rows, ((0, LEFT), (1, MID), (2, RIGHT)), 3) for i in (0, 1)]
+    own += [gather(i, 3, 4, e_rows, ((0, LEFT), (1, RIGHT)), 2) for i in (2, 3)]
 
-    def dst(r):
+    def send(j, e):
+        r = (q + 1 + j) % N
+        k = order(q).index(r)
         rid, pnc, _ = topo.addr(T.cores[r])
-        return DstId(rid=rid, pnc=pnc)
+        need(g, "g", e)
+        for src, dst in ((T.tq[:, 128 * j:128 * j + CAPP].bitcast(dt.uint8), T.rq[:, CAPP * k:CAPP * (k + 1)].bitcast(dt.uint8)),
+                         (T.tc[:, 128 * j:128 * j + CAPP], T.rc[:, CAPP * k:CAPP * (k + 1)])):
+            g.remote_dma(dst, src, s.arrl if k == 2 else s.arre, s.loc, pnc, rid, topo.mask(core, T.cores[r]))
 
-    def send(js, sq, sc, c0, sem):
-        for kind in (0, 1):
-            tr = []
-            for n, j in enumerate(js):
-                r = (q + 1 + j) % N
-                eng = topo.engines(core, T.cores[r])
-                w = len(eng) // len(js)
-                m = sum(1 << x for x in eng[n * w:n * w + w])
-                a, b, at = c0 + n * CAPP, c0 + (n + 1) * CAPP, CAPP * (2 - j)
-                if kind == 0:
-                    sa, da = sq[:, a:b].bitcast(dt.uint8), T.rq[:, at:at + CAPP].bitcast(dt.uint8)
-                else:
-                    sa, da = sc[:, a:b], T.rc[:, at:at + CAPP]
-                tr.append(RemoteDMATransfer(dst_ids=[dst(r)], dma_engine_mask=m, remote_sem=sem, src=sa, dst=da))
-            g.remote_dma_fused(tr, local_sem=s.loc)
-
-    pieces(0)
-    e = quant(T.tq[:], T.tc[:], T.t[:, 0:768])
-    need(g, "g", e)
-    send([0, 1], T.tq, T.tc, 0, s.arre)
-    pieces(1)
-    e = quant(T.tq1[:], T.tc1[:], T.t[:, 640:1152])
-    need(g, "g", e)
-    send([2], T.tq1, T.tc1, 32, s.arrl)
-    pieces(2)
-    e_own = quant(T.tq2[:], T.tc2[:], T.t[:, 1024:1536])
+    for j in cuts:
+        send(j, pieces(j, (3, 3, 2, 2), (g0, g1, got[2, j], got[3, j])))
     vw(("du", 16), ("dv", 16))
     e_uv = quant(T.uvq[:], T.uvc[:], T.uv[:])
+    e_own = pieces(3, (3, 3, 2, 2), own)
 
-    c1 = CAPP * (q + 1)
     vw(("gi", 32))
-    V(v.tensor_scalar(T.pn[:], T.pp[:, 16:32], 0, 1 + c1, A.is_lt, A.mult))
-    e = V(v.tensor_scalar(T.pw[:], T.pp[:], c1, SL, A.is_lt, A.mult))
+    e = V(ts(T.pn[:], T.pp[:, 16:32], 0, SL + 1, A.is_lt, A.mult))
+    e_f = V(v.tensor_copy(T.offf[:], T.pp[:, 0:16]))
     vw(e)
-    e = V(v.tensor_tensor(T.pw[:], T.pw[:], T.pp[:], A.add))
+    e = V(tt(T.pn[:], T.pn[:], T.pp[:, 16:32], A.add))
     vw(e)
-    e_f = V(v.tensor_scalar(T.offf[:], T.pw[:, 0:16], -c1, None, A.add))
-    e = V(v.tensor_tensor(T.pn[:], T.pn[:], T.pw[:, 16:32], A.add))
-    vw(e)
-    e_g = V(v.tensor_scalar(T.offg[:], T.pn[:], -c1, None, A.add))
+    e_g = V(v.tensor_copy(T.offg[:], T.pn[:]))
 
-    def prod(x, xc, n, skip, m, at, bv, bu):
+    def prod(x, xc, n, parts, bv, bu):
         ev_ = mm(bv, n, T.uvq[:, 128:256], T.uvc[:, 128:256], x, xc)
         eu = mm(bu, n, T.uvq[:, 0:128], T.uvc[:, 0:128], x, xc)
-        need(act, "a", ev_)
-        a = S(act.activation(T.zvs[:, at:at + m], T.ps[:, 512 * bv + skip:512 * bv + skip + m], F.Copy))
+        aw(ev_)
         vw(eu)
-        b = V(v.tensor_copy(T.zus[:, at:at + m], T.ps[:, 512 * bu + skip:512 * bu + skip + m]))
+        for c, r in parts:
+            a = S(act.activation(T.zvs[:, CAPP * r:CAPP * (r + 1)], T.ps[:, 512 * bv + c:512 * bv + c + CAPP], F.Copy))
+            b = V(v.tensor_copy(T.zus[:, CAPP * r:CAPP * (r + 1)], T.ps[:, 512 * bu + c:512 * bu + c + CAPP]))
         return a, b
 
-    need(ten, "t", e_own, e_uv)
-    prod(T.tq2[:], T.tc2[:], 128, 32, CAPP, 288, 5, 6)
-    need(ten, "t", ("arre", 16), ev[3])
-    prod(T.rq[:, 96:288], T.rc[:, 96:288], 192, 0, 192, 96, 7, 0)
-    need(ten, "t", ("arrl", 16))
-    a, b = prod(T.rq[:, 0:128], T.rc[:, 0:128], 128, 0, CAPP, 0, 1, 2)
+    frm = [[r for r in range(N) if r != q and order(r).index(q) == k] for k in range(3)]
+    n_eng = [2 * len(topo.engines(T.cores[f[0]], core)) for f in frm]
+    need(ten, "t", e_own, e_uv, h3)
+    prod(T.tq[:, 384:512], T.tc[:, 384:512], 128, [(0, q)], 6, 7)
+    need(ten, "t", ("arre", n_eng[0] + n_eng[1]))
+    prod(T.rq[:, 0:192], T.rc[:, 0:192], 192, [(0, frm[0][0]), (CAPP, frm[1][0])], 0, 1)
+    need(ten, "t", ("arrl", n_eng[2]))
+    a, b = prod(T.rq[:, 160:288], T.rc[:, 160:288], 128, [(32, frm[2][0])], 2, 3)
     H = 96
-    need(act, "a", a, e_f)
+    aw(a, e_f)
     e = S(act.activation(T.y1[:, H:P], T.zvs[:].indirect(T.offf[:, H // 16:P // 16]), F.Copy))
-    vw(a, b, e_g, e3)
+    vw(a, b, e_g)
     vw(V(v.tensor_copy(T.y1[:, 0:H], T.zvs[:].indirect(T.offf[:, 0:H // 16]))))
-    for c, d in ((0, H), (H, P)):
+    for c, d, eng, en in ((0, H, sy, "s"), (H, P, act, "a")):
         if c:
             vw(e)
-        o = V(v.tensor_tensor(T.ys[:, c:d], T.zus[:].indirect(T.offg[:, c // 16:d // 16]), T.y1[:, c:d], A.add))
-        need(sy, "s", o)
-        sy.dma_start(T.y[:, c:d], T.ys[:, c:d]).then_inc(s.dy, 16)
+        o = V(tt(T.ys[:, c:d], T.zus[:].indirect(T.offg[:, c // 16:d // 16]), T.y1[:, c:d], A.add))
+        need(eng, en, o)
+        eng.dma_start(T.y[:, c:d], T.ys[:, c:d]).then_inc(s.dy, 16)
     sy.wait_ge(s.dy, 32)
-    g.wait_ge(s.loc, 32)
+    g.wait_ge(s.loc, sum(2 * len(topo.engines(core, T.cores[r])) for r in order(q)))
     for name in ("sv", "st", "sa", "sg"):
         need(g, "g", (name, cnt[name]))

@@ -8,7 +8,7 @@ CAPP = 96
 P = 256
 SL = N * CAPP
 X = 512
-HALF = X // 2
+QUART, HALF = X // 4, X // 2
 SH = (1, 3, 6)
 BL = (8, 64)
 P64, P8, H0, S8, S64, NT = 0, 1, 2, 3, 4, 5
@@ -23,6 +23,10 @@ B12 = 1616
 PAIR = B12 + 2 * SEC
 LEFT, MID, RIGHT = 0, 1, 2
 REM = 3 * CAPP
+RES = (0, 2, 1, 3)
+WID = (3, 2)
+IDX = (3, 1, 1)
+H = 128
 
 SCRATCH = {
     "xs": ("sbuf", [128, 2048], "bfloat16"),
@@ -35,13 +39,13 @@ SCRATCH = {
     "uvq": ("sbuf", [128, 256], "float8_e4m3fn_x4"),
     "uvc": ("sbuf", [128, 256], "uint8"),
     "ps": ("psum", [128, 4096], "float32"),
-    "tw": ("sbuf", [128, 4 * NT * X], "bfloat16"),
-    "bm": ("sbuf", [128, 4 * NG], "bfloat16"),
+    "tw": ("sbuf", [128, 4, NT * X], "bfloat16"),
+    "bm": ("sbuf", [128, 2, 2 * NG], "bfloat16"),
     "bt": ("sbuf", [128, 2 * PAIR], "bfloat16"),
     "cp": ("sbuf", [128, 2 * X + 72], "bfloat16"),
     "cr": ("sbuf", [128, 14 * NG], "bfloat16"),
-    "mi": ("sbuf", [128, 2 * CAPP], "bfloat16"),
-    "m3": ("sbuf", [128, 3 * CAPP], "bfloat16"),
+    "mi": ("sbuf", [128, 4 * CAPP], "bfloat16"),
+    "m3": ("sbuf", [128, 6 * CAPP], "bfloat16"),
     "lnb": ("sbuf", [128, 24], "int32"),
     "xt": ("sbuf", [128, 2, 24], "int32"),
     "tt": ("sbuf", [128, 3, 2, 24], "int32"),
@@ -50,8 +54,8 @@ SCRATCH = {
     "mm": ("sbuf", [128, 3, 24], "float32"),
     "oo": ("sbuf", [128, 3, 24], "float32"),
     "off": ("sbuf", [128, 3, 24], "uint16"),
-    "ga": ("sbuf", [128, 12 * SL], "bfloat16"),
-    "gb": ("sbuf", [128, 12 * SL], "bfloat16"),
+    "ga": ("sbuf", [128, 2, 6 * SL], "bfloat16"),
+    "gb": ("sbuf", [128, 2, 6 * SL], "bfloat16"),
     "t": ("sbuf", [128, N, 512], "bfloat16"),
     "tq": ("sbuf", [128, 512], "float8_e4m3fn_x4"),
     "tc": ("sbuf", [128, 512], "uint8"),
@@ -60,15 +64,13 @@ SCRATCH = {
     "pidx": ("sbuf", [128, 1], "int32"),
     "pid16": ("sbuf", [128, 1], "int32"),
     "pp": ("sbuf", [128, 32], "int32"),
-    "pn": ("sbuf", [128, 16], "float32"),
-    "offf": ("sbuf", [128, 16], "uint16"),
-    "offg": ("sbuf", [128, 16], "uint16"),
-    "zvs": ("sbuf", [128, SL], "float32"),
-    "zus": ("sbuf", [128, SL + 8], "float32"),
+    "offp": ("sbuf", [128, 32], "uint16"),
+    "zvs": ("sbuf", [128, SL + 1], "float32"),
+    "zus": ("sbuf", [128, SL + 1], "float32"),
     "y1": ("sbuf", [128, P], "float32"),
     "ys": ("sbuf", [128, P], "float32"),
 }
-SEMAPHORES = ["sv", "st", "sa", "sg", "dlo", "dln", "dx0", "dx1", "da0", "da1", "da2", "du", "dv", "dy",
+SEMAPHORES = ["sv", "st", "sa", "sg", "dlo", "dln", "dx0", "dx1", "dx2", "da0", "da1", "da2", "da3", "du", "dv", "dy",
               "gi", "arre", "arrl", "loc"]
 
 
@@ -110,27 +112,33 @@ def rank_program(g, core, T, topo):
         far = [(r + 1 + j) % N for j in range(N - 1)]
         return sorted(far, key=lambda k: topo.same_plane(topo.chip(T.cores[r]), topo.chip(T.cores[k])))
 
-    sy.dma_start(T.xt[:, 0], T.lo[:]).then_inc(s.dlo, 16)
+    def load_a(eng, i):
+        eng.dma_start(T.ab[:, 512 * i:512 * i + 512], T.a[:, 512 * RES[i]:512 * RES[i] + 512]).then_inc(s["da%d" % i], 16)
+
+    def load_x(a, b, sem):
+        sy.dma_start(T.xs[:, 4 * a:4 * b], T.x[:, 4 * a:4 * b]).then_inc(sem, 16)
+
+    load_a(act, 0)
+    load_x(0, HALF, s.dx0)
     act.dma_start(T.lnb[:], T.ln[:]).then_inc(s.dln, 16)
-    act.dma_start(T.ab[:, 0:512], T.a[:, 0:512]).then_inc(s.da0, 16)
-    sy.dma_start(T.xs[:, 0:1024], T.x[:, 0:1024]).then_inc(s.dx0, 16)
-    act.dma_start(T.ab[:, 512:1024], T.a[:, 512:1024]).then_inc(s.da1, 16)
-    sy.dma_start(T.xs[:, 1024:2048], T.x[:, 1024:2048]).then_inc(s.dx1, 16)
-    sy.dma_start(T.ab[:, 1024:2048], T.a[:, 1024:2048]).then_inc(s.da2, 16)
+    sy.dma_start(T.xt[:, 0], T.lo[:]).then_inc(s.dlo, 16)
+    load_a(act, 1)
+    load_x(HALF, X, s.dx1)
+    load_a(sy, 2)
+    load_a(sy, 3)
     sy.dma_start(T.uv[:, 0:512], T.u[:]).then_inc(s.du, 16)
     sy.dma_start(T.uv[:, 512:1024], T.v[:]).then_inc(s.dv, 16)
 
     e_iota = G(g.iota(T.pidx[:], [[0, 1]], 0, 1))
     CP = (0, X + 8)
     e = V(v.memset(T.cp[:], BIG))
-    e_big = V(v.memset(T.m3[:], BIG))
-    V(v.memset(T.zus[:, SL:SL + 8], 0.0))
+    V(v.memset(T.zus[:, 0:1], 0.0))
     vw(e_iota)
     e_pid = V(v.tensor_scalar(T.pid16[:], T.pidx[:], 15, None, A.bitwise_and))
-    vw(e_big)
-    V(v.memset(T.m3[:, 0:3 * CAPP:3], 0.0))
+    vw(e)
     for n, b in enumerate(BL):
         e_cp = V(v.memset(T.cp[:, CP[n]:CP[n] + X + b:b], 0.0))
+    e_big = V(v.memset(T.m3[:], BIG))
     aw(e_cp)
     e_cr = S(act.activation(T.cr[:], T.cp[:, 0:14 * NG], F.Identity, bias=BIG, scale=0.0))
 
@@ -143,10 +151,14 @@ def rank_program(g, core, T, topo):
         return zeros(T.bt[:, o + B12 + 7:o + PAIR:8], 2 * NG)
 
     e_bz = [clear(0)]
-    G(g.iota(T.mi[:], [[0, CAPP], [1, 2]], 0, 0, allow_small_or_imprecise_dtypes=True))
+    G(g.iota(T.mi[:], [[0, 2 * CAPP], [1, 2]], 0, 0, allow_small_or_imprecise_dtypes=True))
     e_t = G(g.iota(T.t[:, :, 4 * CAPP:512], [[0, N], [0, 128]], 0, 0, allow_small_or_imprecise_dtypes=True))
     need(g, "g", e_cr)
     e_cr = G(g.affine_select(T.cr[:], T.cr[:], [[-1, 7], [0, NG // 4], [1, 8]], A.is_gt, 0.0, 0, 0))
+    G(g.iota(T.bt[:, PAIR + Z0:PAIR + B12:2], [[0, (B12 - Z0) // 2]], 0, 0, allow_small_or_imprecise_dtypes=True))
+    need(g, "g", e_big)
+    G(g.iota(T.m3[:, 0:6 * CAPP:3], [[0, 2 * CAPP]], 0, 0, allow_small_or_imprecise_dtypes=True))
+    e_bz.append(G(g.iota(T.bt[:, PAIR + B12 + 7:2 * PAIR:8], [[0, 2 * NG]], 0, 0, allow_small_or_imprecise_dtypes=True)))
     need(g, "g", e_pid)
     for n, tab in enumerate((T.pf, T.pg)):
         g.indirect_dma_start(T.pp[:, 16 * n:16 * n + 16], None, tab[:], IndirectOffsetOnAxis(ap=T.pid16[:, 0:1], axis=0),
@@ -187,12 +199,10 @@ def rank_program(g, core, T, topo):
         return done(ten.matmul_mx(T.ps[:, 512 * bank:512 * bank + n], w, wc, x, xc, True, True), "st")
 
     def col(i, t, a=0, b=X, st=1):
-        o = X * (NT * i + t)
-        return T.tw[:, o + a:o + b:st]
+        return T.tw[:, i, X * t + a:X * t + b:st]
 
     def back(i, t, a, b):
-        o = X * (NT * i + t)
-        return T.tw[:, o + b - 1:o + a - 1:-1]
+        return T.tw[:, i, X * t + b - 1:X * t + a - 1:-1]
 
     def make_h(i, a, b, bank, e):
         need(ten, "t", e)
@@ -200,8 +210,8 @@ def rank_program(g, core, T, topo):
         aw(z)
         return S(act.activation(col(i, H0, a, b), T.ps[:, 512 * bank:512 * bank + b - a], F.Relu, scale=0.05))
 
-    def quant_a(i0, i1, sem):
-        vw((sem, 16))
+    def quant_a(i0, i1):
+        vw(*[("da%d" % i, 16) for i in range(i0, i1)])
         return quant(T.aq[:, 128 * i0:128 * i1], T.ac[:, 128 * i0:128 * i1], T.ab[:, 512 * i0:512 * i1])
 
     def quant_x(a, b, sem):
@@ -214,116 +224,127 @@ def rank_program(g, core, T, topo):
         return e
 
     def scan_p(i, a=0, b=X):
+        if a:
+            vw(upto[i])
         for n in (0, 1):
             first = col(i, PT[n], a - 1, a) if a else 0.0
-            e = V(v.tensor_tensor_scan(col(i, PT[n], a, b), col(i, H0, a, b), T.cp[:, CP[n] + 2:CP[n] + 2 + b - a],
-                                       first, A.max, A.min))
-        return e
+            upto[i] = V(v.tensor_tensor_scan(col(i, PT[n], a, b), col(i, H0, a, b), T.cp[:, CP[n] + 2:CP[n] + 2 + b - a],
+                                             first, A.max, A.min))
+        return upto[i]
+
+    upto = {}
 
     def inner(i, k):
         o = PAIR * (i // 2) + SEC * (i % 2) + C0 - k
         return T.bt[:, o:o - X:-8]
 
-    def pairs(i):
-        vw(e_bz[i // 2])
-        V(tt(inner(i, 6), col(i, H0, 1, X, 8), col(i, H0, 2, X, 8), A.max))
-        return V(tt(inner(i, 8), col(i, H0, 3, X, 8), col(i, H0, 4, X, 8), A.max))
-
-    def blocks(i):
-        o = NG * i
-        V(tt(T.bm[:, o:o + 64], col(i, P8, 5, X, 8), col(i, H0, 6, X, 8), A.max))
-        return V(tt(T.bm[:, o + 64:o + NG], col(i, P64, 61, X, 64), col(i, H0, 62, X, 64), A.max))
-
     def middles(p):
         i, o = 2 * p, PAIR * p + B12
-        e = pairs(i)
-        vw(e)
-        blocks(i)
-        e = pairs(i + 1)
-        f = blocks(i + 1)
+        vw(e_bz[p])
+        for k in (i, i + 1):
+            V(tt(inner(k, 6), col(k, H0, 1, X, 8), col(k, H0, 2, X, 8), A.max))
+            e = V(tt(inner(k, 8), col(k, H0, 3, X, 8), col(k, H0, 4, X, 8), A.max))
+            if k == i:
+                first = e
+        vw(first)
+        for k in (i, i + 1):
+            for n, b in enumerate(BL):
+                c = NG * (k - i) + 64 * n
+                f = V(tt(T.bm[:, p, c:c + X // b], col(k, PT[n], b - 3, X, b), col(k, H0, b - 2, X, b), A.max))
         vw(e)
         for k in (i, i + 1):
             V(tt(inner(k, 9), inner(k, 6), inner(k, 8), A.max))
         vw(f, e_cr)
         for a in range(7):
-            e = V(v.tensor_tensor_scan(T.bt[:, o + a:o + 2 * SEC:8], T.bm[:, 2 * NG * p:2 * NG * (p + 1)],
-                                       T.cr[:, 2 * NG * a:2 * NG * (a + 1)], 0.0, A.max, A.min))
+            e = V(v.tensor_tensor_scan(T.bt[:, o + a:o + 2 * SEC:8], T.bm[:, p], T.cr[:, 2 * NG * a:2 * NG * (a + 1)],
+                                       0.0, A.max, A.min))
         return e
 
     def win(i, n):
         if n == MID:
             o = PAIR * (i // 2)
             return T.bt[:, o + SEC * (i % 2):o + PAIR]
-        o = X * (NT * i + (H0 if n == LEFT else P64))
-        return T.tw[:, o:o + 3 * X]
+        o = X * (H0 if n == LEFT else P64)
+        return T.tw[:, i, o:o + 3 * X]
 
     def off(n, j0, j1):
         return T.off[:, n, 6 * j0:6 * j1]
 
-    def gather(i, j0, j1, after, ns, w):
-        o = 3 * SL * i
-        for k, n in ns:
+    def gather(i, j0, j1, after, *ns):
+        w = WID[i // 2]
+        for n in ns:
             aw(after, e_off)
-            e = S(act.activation(T.ga[:, o + w * CAPP * j0 + k:o + w * CAPP * j1:w], win(i, n).indirect(off(n, j0, j1)), F.Copy))
+            k = w * (i % 2) + min(n, w - 1)
+            e = S(act.activation(T.ga[:, i // 2, 2 * w * CAPP * j0 + k:2 * w * CAPP * j1:2 * w],
+                                 win(i, n).indirect(off(n, j0, j1)), F.Copy))
         return e
 
-    def largest(i, j, w, e):
+    def largest(p, j, e):
         vw(e)
-        o, n = 3 * SL * i + w * CAPP * j, w * CAPP
-        mask, op = (T.mi, A.mult) if w == 2 else (T.m3, A.min)
-        return V(v.tensor_tensor_scan(T.gb[:, o:o + n], mask[:], T.ga[:, o:o + n], 0.0, op, A.max))
+        n = 2 * WID[p] * CAPP
+        mask, op = ((T.m3, A.min), (T.mi, A.mult))[p]
+        return V(v.tensor_tensor_scan(T.gb[:, p, n * j:n * j + n], mask[:], T.ga[:, p, n * j:n * j + n], 0.0, op, A.max))
 
-    def finish(i, j, w, e):
+    def take(j, e):
+        need(g, "g", e)
+        return G(g.affine_select(T.t[:, j, 0:4 * CAPP:2], T.gb[:, 0, 6 * CAPP * j + 2:6 * CAPP * (j + 1):3],
+                                 [[0, 2 * CAPP]], A.is_equal, 0.0, 0, 0))
+
+    def copy3(j, e):
         vw(e)
-        o = 3 * SL * i + w * CAPP * j
-        last, piece = T.gb[:, o + w - 1:o + w * CAPP:w], T.t[:, j, i:4 * CAPP:4]
-        if w == 3:
-            return V(v.tensor_copy(piece, last))
-        return V(tt(piece, win(i, MID).indirect(off(MID, j, j + 1)), last, A.max))
+        return V(v.tensor_copy(T.t[:, j, 0:4 * CAPP:2], T.gb[:, 0, 6 * CAPP * j + 2:6 * CAPP * (j + 1):3]))
 
-    def pieces(j, ws, es):
-        big = [largest(i, j, ws[i], es[i]) for i in range(4)]
-        for i in range(4):
-            e = finish(i, j, ws[i], big[i])
-        vw(e, e_t)
+    def second(buf, i, j):
+        return buf[:, 1, 4 * CAPP * j + RES[i]:4 * CAPP * (j + 1):4]
+
+    def joins(j, e):
+        vw(e)
+        for i in (2, 3):
+            e = V(tt(T.t[:, j, RES[i]:4 * CAPP:4], win(i, MID).indirect(off(MID, j, j + 1)), second(T.gb, i, j), A.max))
+        return e
+
+    def codes(j, *es):
+        vw(e_t, *es)
         return quant(T.tq[:, 128 * j:128 * j + 128], T.tc[:, 128 * j:128 * j + 128], T.t[:, j])
 
     cuts = [(r - q - 1) % N for r in order(q)]
-    index(4)
-    quant_a(0, 1, "da0")
-    e = quant_x(0, HALF, "dx0")
-    h00 = make_h(0, 0, HALF, 0, e)
-    h10 = make_h(1, 0, HALF, 1, quant_a(1, 2, "da1"))
-    e_bz.append(clear(1))
-    index(3)
+    quant_a(0, 1)
+    h00 = make_h(0, 0, HALF, 0, quant_x(0, HALF, "dx0"))
+    index(IDX[0])
+    h10 = make_h(1, 0, HALF, 1, quant_a(1, 2))
+    index(IDX[1])
     vw(e_cp, h00)
     scan_p(0, 0, HALF)
-    scan_s(0, 0, HALF)
+    index(1)
     e = quant_x(HALF, X, "dx1")
     h01 = make_h(0, HALF, X, 2, e)
     h11 = make_h(1, HALF, X, 3, e)
     index(1)
+    scan_s(0, 0, HALF)
+    index(1)
     vw(h10)
     scan_p(1, 0, HALF)
     index(1)
-    scan_s(1, 0, HALF)
-    e_off = index(1)
+    if IDX[2]:
+        scan_s(1, 0, HALF)
+    index(9 - at["step"])
     vw(h01)
     e = scan_s(0, HALF, X)
-    gather(0, 0, 3, e, ((0, LEFT),), 3)
+    e_off = index(1)
+    gather(0, 0, 3, e, LEFT)
     e = scan_p(0, HALF, X)
-    gather(0, 0, 3, e, ((2, RIGHT),), 3)
-    e = quant_a(2, 4, "da2")
-    h2 = make_h(2, 0, X, 4, e)
-    h3 = make_h(3, 0, X, 5, e)
+    gather(0, 0, 3, e, RIGHT)
+    e2 = quant_a(2, 4)
+    h2 = make_h(2, 0, X, 4, e2)
     vw(h11)
-    e = scan_s(1, HALF, X)
-    gather(1, 0, 3, e, ((0, LEFT),), 3)
+    e = scan_s(1, HALF if IDX[2] else 0, X)
+    gather(1, 0, 3, e, LEFT)
+    h3 = make_h(3, 0, X, 5, e2)
     e = scan_p(1, HALF, X)
-    gather(1, 0, 3, e, ((2, RIGHT),), 3)
+    gather(1, 0, 3, e, RIGHT)
     e = middles(0)
-    g0 = gather(0, 0, 3, e, ((1, MID),), 3)
-    g1 = gather(1, 0, 3, e, ((1, MID),), 3)
+    gather(0, 0, 3, e, MID)
+    g0 = gather(1, 0, 3, e, MID)
     ends = {}
     for i, h in ((2, h2), (3, h3)):
         vw(h)
@@ -331,12 +352,13 @@ def rank_program(g, core, T, topo):
         ends[i] = (es, scan_p(i))
     e_rows = middles(1)
     got = {}
-    for j in cuts:
+    for js in (cuts[:1], sorted(cuts[1:])):
         for i in (2, 3):
-            gather(i, j, j + 1, ends[i][0], ((0, LEFT),), 2)
-            got[i, j] = gather(i, j, j + 1, ends[i][1], ((1, RIGHT),), 2)
-    own = [gather(i, 3, 4, e_rows, ((0, LEFT), (1, MID), (2, RIGHT)), 3) for i in (0, 1)]
-    own += [gather(i, 3, 4, e_rows, ((0, LEFT), (1, RIGHT)), 2) for i in (2, 3)]
+            gather(i, js[0], js[-1] + 1, ends[i][0], LEFT)
+            e = gather(i, js[0], js[-1] + 1, ends[i][1], RIGHT)
+        got.update({j: e for j in js})
+    own0 = [gather(i, 3, 4, e_rows, LEFT, MID, RIGHT) for i in (0, 1)][-1]
+    own1 = [gather(i, 3, 4, e_rows, LEFT, RIGHT) for i in (2, 3)][-1]
 
     def send(j, e):
         r = (q + 1 + j) % N
@@ -347,47 +369,59 @@ def rank_program(g, core, T, topo):
                          (T.tc[:, 128 * j:128 * j + CAPP], T.rc[:, CAPP * k:CAPP * (k + 1)])):
             g.remote_dma(dst, src, s.arrl if k == 2 else s.arre, s.loc, pnc, rid, topo.mask(core, T.cores[r]))
 
-    for j in cuts:
-        send(j, pieces(j, (3, 3, 2, 2), (g0, g1, got[2, j], got[3, j])))
+    ja, jb, jc = cuts
+    ta = take(ja, largest(0, ja, g0))
+    a = largest(1, ja, got[ja])
+    tb = take(jb, largest(0, jb, g0))
+    send(ja, codes(ja, joins(ja, a), ta))
+    c = largest(0, jc, g0)
+    b = largest(1, jb, got[jb])
+    vw(("gi", 32))
+    e_p = V(ts(T.offp[:], T.pp[:], 1, None, A.add))
+    e = joins(jb, b)
+    c = largest(1, jc, got[jc]), c
+    send(jb, codes(jb, e, tb))
+    joins(jc, c[0])
+    send(jc, codes(jc, copy3(jc, c[1])))
+    a = largest(0, 3, own0)
     vw(("du", 16), ("dv", 16))
     e_uv = quant(T.uvq[:], T.uvc[:], T.uv[:])
-    e_own = pieces(3, (3, 3, 2, 2), own)
+    b = largest(1, 3, own1)
+    copy3(3, a)
+    e_own = codes(3, joins(3, b))
 
-    vw(("gi", 32))
-    e = V(ts(T.pn[:], T.pp[:, 16:32], 0, SL + 1, A.is_lt, A.mult))
-    e_f = V(v.tensor_copy(T.offf[:], T.pp[:, 0:16]))
-    vw(e)
-    e = V(tt(T.pn[:], T.pn[:], T.pp[:, 16:32], A.add))
-    vw(e)
-    e_g = V(v.tensor_copy(T.offg[:], T.pn[:]))
-
-    def prod(x, xc, n, parts, bv, bu):
-        ev_ = mm(bv, n, T.uvq[:, 128:256], T.uvc[:, 128:256], x, xc)
+    def prod(x, xc, n, parts, bv, bu, both):
         eu = mm(bu, n, T.uvq[:, 0:128], T.uvc[:, 0:128], x, xc)
-        aw(ev_)
-        vw(eu)
+        ev_ = mm(bv, n, T.uvq[:, 128:256], T.uvc[:, 128:256], x, xc)
         for c, r in parts:
-            a = S(act.activation(T.zvs[:, CAPP * r:CAPP * (r + 1)], T.ps[:, 512 * bv + c:512 * bv + c + CAPP], F.Copy))
-            b = V(v.tensor_copy(T.zus[:, CAPP * r:CAPP * (r + 1)], T.ps[:, 512 * bu + c:512 * bu + c + CAPP]))
+            aw(ev_)
+            a = S(act.activation(T.zvs[:, CAPP * r + 1:CAPP * (r + 1) + 1], T.ps[:, 512 * bv + c:512 * bv + c + CAPP], F.Copy))
+        for c, r in parts:
+            to, fr = T.zus[:, CAPP * r + 1:CAPP * (r + 1) + 1], T.ps[:, 512 * bu + c:512 * bu + c + CAPP]
+            if both:
+                aw(eu)
+                b = S(act.activation(to, fr, F.Copy))
+            else:
+                vw(eu)
+                b = V(v.tensor_copy(to, fr))
         return a, b
 
-    frm = [[r for r in range(N) if r != q and order(r).index(q) == k] for k in range(3)]
-    n_eng = [2 * len(topo.engines(T.cores[f[0]], core)) for f in frm]
-    need(ten, "t", e_own, e_uv, h3)
-    prod(T.tq[:, 384:512], T.tc[:, 384:512], 128, [(0, q)], 6, 7)
-    need(ten, "t", ("arre", n_eng[0] + n_eng[1]))
-    prod(T.rq[:, 0:192], T.rc[:, 0:192], 192, [(0, frm[0][0]), (CAPP, frm[1][0])], 0, 1)
+    frm = [[r for r in range(N) if r != q and order(r).index(q) == k][0] for k in range(3)]
+    n_eng = [2 * len(topo.engines(T.cores[r], core)) for r in frm]
+    need(ten, "t", e_uv, h3, ("arre", n_eng[0] + n_eng[1]))
+    _, e_early = prod(T.rq[:, 0:192], T.rc[:, 0:192], 192, [(0, frm[0]), (CAPP, frm[1])], 0, 1, True)
+    need(ten, "t", e_own)
+    prod(T.tq[:, 384:512], T.tc[:, 384:512], 128, [(0, q)], 2, 3, False)
     need(ten, "t", ("arrl", n_eng[2]))
-    a, b = prod(T.rq[:, 160:288], T.rc[:, 160:288], 128, [(32, frm[2][0])], 2, 3)
-    H = 96
-    aw(a, e_f)
-    e = S(act.activation(T.y1[:, H:P], T.zvs[:].indirect(T.offf[:, H // 16:P // 16]), F.Copy))
-    vw(a, b, e_g)
-    vw(V(v.tensor_copy(T.y1[:, 0:H], T.zvs[:].indirect(T.offf[:, 0:H // 16]))))
+    a, b = prod(T.rq[:, 160:288], T.rc[:, 160:288], 128, [(32, frm[2])], 4, 5, False)
+    aw(a, e_p)
+    e = S(act.activation(T.y1[:, H:P], T.zvs[:].indirect(T.offp[:, H // 16:P // 16]), F.Copy))
+    vw(b, e_early)
+    f = V(v.tensor_copy(T.y1[:, 0:H], T.zus[:].indirect(T.offp[:, P // 16:(P + H) // 16])))
     for c, d, eng, en in ((0, H, sy, "s"), (H, P, act, "a")):
-        if c:
-            vw(e)
-        o = V(tt(T.ys[:, c:d], T.zus[:].indirect(T.offg[:, c // 16:d // 16]), T.y1[:, c:d], A.add))
+        vw(*((e,) if c else (f, a)))
+        w, k = (T.zus, P) if c else (T.zvs, 0)
+        o = V(tt(T.ys[:, c:d], w[:].indirect(T.offp[:, (k + c) // 16:(k + d) // 16]), T.y1[:, c:d], A.add))
         need(eng, en, o)
         eng.dma_start(T.y[:, c:d], T.ys[:, c:d]).then_inc(s.dy, 16)
     sy.wait_ge(s.dy, 32)

@@ -11,21 +11,22 @@ X = 512
 QUART, HALF = X // 4, X // 2
 SH = (1, 3, 6)
 BL = (8, 64)
-P64, P8, H0, S8, S64, NT = 0, 1, 2, 3, 4, 5
-PT = (P8, P64)
+P8, H0, S8, S64, NT = 0, 1, 2, 3, 4
 ST = (S8, S64)
 BIG = 1e29
-NG = X // 8 + 8
-SEC = 8 * NG
+NG = 2 * X // 8
 C0 = 1041
 Z0 = C0 - X - 1
-B12 = 1616
-PAIR = B12 + 2 * SEC
+B1 = Z0 + 2 * X
+B2 = B1 + 2 * X
+PAIR = B2 + 2 * X
 LEFT, MID, RIGHT = 0, 1, 2
 REM = 3 * CAPP
 RES = (0, 2, 1, 3)
 WID = (3, 2)
-IDX = (3, 1, 1)
+PLAN = "i3 a0 i1 x0 h00 i1 a1 h10 i1 x1 h01 h11 i1 P00 a2 h20 h21 i1 S00 a3 h30 h31 i1 S01 i1 P01 R0 L0 S1 P1 L1 R1"
+LOADS = ("ln a0 a1 a2", "lo x0 x1 a3", "")
+LATE = 0
 H = 128
 
 SCRATCH = {
@@ -40,27 +41,25 @@ SCRATCH = {
     "uvc": ("sbuf", [128, 256], "uint8"),
     "ps": ("psum", [128, 4096], "float32"),
     "tw": ("sbuf", [128, 4, NT * X], "bfloat16"),
-    "bm": ("sbuf", [128, 2, 2 * NG], "bfloat16"),
+    "bm": ("sbuf", [128, 2, NG], "bfloat16"),
     "bt": ("sbuf", [128, 2 * PAIR], "bfloat16"),
-    "cp": ("sbuf", [128, 2 * X + 72], "bfloat16"),
-    "cr": ("sbuf", [128, 14 * NG], "bfloat16"),
+    "cp": ("sbuf", [128, 2 * X + 8], "bfloat16"),
+    "cr": ("sbuf", [128, 12 * NG], "bfloat16"),
     "mi": ("sbuf", [128, 4 * CAPP], "bfloat16"),
-    "m3": ("sbuf", [128, 6 * CAPP], "bfloat16"),
+    "m3": ("sbuf", [128, 7 * NG], "bfloat16"),
     "lnb": ("sbuf", [128, 24], "int32"),
     "xt": ("sbuf", [128, 2, 24], "int32"),
     "tt": ("sbuf", [128, 3, 2, 24], "int32"),
     "gg": ("sbuf", [128, 2, 24], "float32"),
-    "gs": ("sbuf", [128, 24], "float32"),
+    "gs": ("sbuf", [128, 2, 24], "float32"),
     "mm": ("sbuf", [128, 3, 24], "float32"),
     "oo": ("sbuf", [128, 3, 24], "float32"),
     "off": ("sbuf", [128, 3, 24], "uint16"),
-    "ga": ("sbuf", [128, 2, 6 * SL], "bfloat16"),
-    "gb": ("sbuf", [128, 2, 6 * SL], "bfloat16"),
+    "ga": ("sbuf", [128, 3, 6 * SL], "bfloat16"),
+    "gb": ("sbuf", [128, 3, 6 * SL], "bfloat16"),
     "t": ("sbuf", [128, N, 512], "bfloat16"),
-    "tq": ("sbuf", [128, 512], "float8_e4m3fn_x4"),
-    "tc": ("sbuf", [128, 512], "uint8"),
-    "rq": ("sbuf", [128, REM], "float8_e4m3fn_x4"),
-    "rc": ("sbuf", [128, REM], "uint8"),
+    "tq": ("sbuf", [128, 512 + REM], "float8_e4m3fn_x4"),
+    "tc": ("sbuf", [128, 512 + REM], "uint8"),
     "pidx": ("sbuf", [128, 1], "int32"),
     "pid16": ("sbuf", [128, 1], "int32"),
     "pp": ("sbuf", [128, 32], "int32"),
@@ -70,8 +69,8 @@ SCRATCH = {
     "y1": ("sbuf", [128, P], "float32"),
     "ys": ("sbuf", [128, P], "float32"),
 }
-SEMAPHORES = ["sv", "st", "sa", "sg", "dlo", "dln", "dx0", "dx1", "dx2", "da0", "da1", "da2", "da3", "du", "dv", "dy",
-              "gi", "arre", "arrl", "loc"]
+SEMAPHORES = ["sv", "st", "sa", "sg", "dlo", "dln", "dx0", "dx1", "dx2", "dx3", "dx4", "dx5", "dx6", "da0", "da1", "da2", "da3", "du", "dv", "dy",
+              "gi", "ar0", "ar1", "ar2", "loc"]
 
 
 def rank_program(g, core, T, topo):
@@ -118,69 +117,70 @@ def rank_program(g, core, T, topo):
     def load_x(a, b, sem):
         sy.dma_start(T.xs[:, 4 * a:4 * b], T.x[:, 4 * a:4 * b]).then_inc(sem, 16)
 
-    load_a(act, 0)
-    load_x(0, HALF, s.dx0)
-    act.dma_start(T.lnb[:], T.ln[:]).then_inc(s.dln, 16)
-    sy.dma_start(T.xt[:, 0], T.lo[:]).then_inc(s.dlo, 16)
-    load_a(act, 1)
-    load_x(HALF, X, s.dx1)
-    load_a(sy, 2)
-    load_a(sy, 3)
+    part = {"0": (0, HALF), "1": (HALF, X), "": (0, X), "2": (0, QUART), "3": (QUART, HALF), "4": (QUART, X),
+            "5": (HALF, HALF + QUART), "6": (HALF + QUART, X)}
+    for eng, names in zip((act, sy, g), LOADS):
+        for name in names.split():
+            if name == "ln":
+                eng.dma_start(T.lnb[:], T.ln[:]).then_inc(s.dln, 16)
+            elif name == "lo":
+                eng.dma_start(T.xt[:, 0], T.lo[:]).then_inc(s.dlo, 16)
+            elif name[0] == "a":
+                load_a(eng, int(name[1]))
+            else:
+                a, b = part[name[1]]
+                eng.dma_start(T.xs[:, 4 * a:4 * b], T.x[:, 4 * a:4 * b]).then_inc(s["d" + name], 16)
     sy.dma_start(T.uv[:, 0:512], T.u[:]).then_inc(s.du, 16)
     sy.dma_start(T.uv[:, 512:1024], T.v[:]).then_inc(s.dv, 16)
+    for k in range(4):
+        sy.dma_start(T.pp[16 * (k // 2):16 * (k // 2) + 16, 16 * (k % 2):16 * (k % 2) + 16], (T.pf, T.pg)[k % 2][:]).then_inc(s.gi, 16)
+    for k, n in enumerate((32, 64)):
+        sy.wait_ge(s.gi, 64 + 16 * k)
+        sy.dma_start(T.pp[n:2 * n], T.pp[0:n]).then_inc(s.gi, 16)
 
-    e_iota = G(g.iota(T.pidx[:], [[0, 1]], 0, 1))
     CP = (0, X + 8)
+    e_big = V(v.memset(T.m3[:], BIG))
     e = V(v.memset(T.cp[:], BIG))
     V(v.memset(T.zus[:, 0:1], 0.0))
-    vw(e_iota)
-    e_pid = V(v.tensor_scalar(T.pid16[:], T.pidx[:], 15, None, A.bitwise_and))
     vw(e)
     for n, b in enumerate(BL):
-        e_cp = V(v.memset(T.cp[:, CP[n]:CP[n] + X + b:b], 0.0))
-    e_big = V(v.memset(T.m3[:], BIG))
+        e_cp = V(v.memset(T.cp[:, CP[n]:CP[n] + X + 8 - 8 * n:b], 0.0))
     aw(e_cp)
-    e_cr = S(act.activation(T.cr[:], T.cp[:, 0:14 * NG], F.Identity, bias=BIG, scale=0.0))
+    e_bz = [S(act.activation(T.bt[:, PAIR * p + Z0:PAIR * p + B1:2], T.cp[:, 0:X], F.Copy, scale=0.0)) for p in (0, 1)]
+    e_t = S(act.activation(T.t[:, :, 4 * CAPP:512], T.cp[:, 0:X], F.Copy, scale=0.0))
 
-    def zeros(out, n):
-        return S(act.activation(out, T.cp[:, 0:n], F.Copy, scale=0.0))
+    def fill(out, pattern):
+        return G(g.iota(out, pattern, 0, 0, allow_small_or_imprecise_dtypes=True))
 
-    def clear(p):
-        o = PAIR * p
-        zeros(T.bt[:, o + Z0:o + B12:2], (B12 - Z0) // 2)
-        return zeros(T.bt[:, o + B12 + 7:o + PAIR:8], 2 * NG)
-
-    e_bz = [clear(0)]
-    G(g.iota(T.mi[:], [[0, 2 * CAPP], [1, 2]], 0, 0, allow_small_or_imprecise_dtypes=True))
-    e_t = G(g.iota(T.t[:, :, 4 * CAPP:512], [[0, N], [0, 128]], 0, 0, allow_small_or_imprecise_dtypes=True))
-    need(g, "g", e_cr)
-    e_cr = G(g.affine_select(T.cr[:], T.cr[:], [[-1, 7], [0, NG // 4], [1, 8]], A.is_gt, 0.0, 0, 0))
-    G(g.iota(T.bt[:, PAIR + Z0:PAIR + B12:2], [[0, (B12 - Z0) // 2]], 0, 0, allow_small_or_imprecise_dtypes=True))
     need(g, "g", e_big)
-    G(g.iota(T.m3[:, 0:6 * CAPP:3], [[0, 2 * CAPP]], 0, 0, allow_small_or_imprecise_dtypes=True))
-    e_bz.append(G(g.iota(T.bt[:, PAIR + B12 + 7:2 * PAIR:8], [[0, 2 * NG]], 0, 0, allow_small_or_imprecise_dtypes=True)))
-    need(g, "g", e_pid)
-    for n, tab in enumerate((T.pf, T.pg)):
-        g.indirect_dma_start(T.pp[:, 16 * n:16 * n + 16], None, tab[:], IndirectOffsetOnAxis(ap=T.pid16[:, 0:1], axis=0),
-                             bounds_check=15).then_inc(s.gi, 16)
+    G(g.affine_select(T.cr[:, 0:5 * NG], T.m3[:, 0:5 * NG], [[-1, 5], [0, NG // 8], [1, 8]], A.is_gt, 0.0, 0, 0))
+    e_cr = G(g.affine_select(T.cr[:, 5 * NG:12 * NG], T.m3[:], [[-8, 7], [0, 2], [1, NG // 2]], A.is_ge, 0.0, -8, 0))
+    for o in (0, PAIR):
+        fill(T.bt[:, o + B1 + 45:o + B2:64], [[0, NG // 8]])
+        fill(T.bt[:, o + B1 + 54:o + B2:64], [[0, NG // 8]])
+        fill(T.bt[:, o + B1 + 7:o + PAIR:8], [[0, 2 * NG]])
+    fill(T.mi[:], [[0, 2 * CAPP], [1, 2]])
+    need(g, "g", e_cr)
+    e_m3 = fill(T.m3[:, 0:6 * CAPP:3], [[0, 2 * CAPP]])
 
     m = 6 * ((q + 1) % N)
     runs = [(0, m, 24)] + ([(24 - m, 0, m)] if m else [])
     ts, tt = v.tensor_scalar, v.tensor_tensor
-    base = (C0, B12 - 8, B12 - 8 + 8 * (X // 8))
+    base = (C0, B1 - 8, B2 - 8)
+    D = (X - 2) / 3.0
     steps = [
         [lambda: tt(T.xt[:, 1], T.xt[:, 0], T.lnb[:], A.add)],
         [lambda: ts(T.xt[:, 1], T.xt[:, 1], 1, None, A.add)],
         [lambda k=k: ts(T.tt[:, k], T.xt[:], SH[k], None, A.arith_shift_right) for k in (1, 2, 0)],
         [lambda: tt(T.gg[:], T.tt[:, 1:3, 1], T.tt[:, 1:3, 0], A.is_gt)]
-        + [lambda k=k: ts(T.mm[:, k], T.tt[:, k, 1], (-3.0, 8.0, 8.0)[k], float(base[k] - X + 1), A.mult, A.add) for k in range(3)],
-        [lambda: tt(T.gs[:], T.gg[:, 0], T.gg[:, 1], A.add), lambda: ts(T.tt[:, 1, 0], T.tt[:, 1, 0], 7, None, A.bitwise_and)],
-        [lambda: ts(T.gs[:], T.gs[:], float(X), float(1 - X), A.mult, A.add), lambda: tt(T.mm[:], T.mm[:], T.tt[:, :, 0], A.add)],
-        [lambda: tt(T.mm[:, 1:3], T.mm[:, 1:3], T.gg[:], A.mult), lambda: tt(T.oo[:, LEFT], T.xt[:, 0], T.gs[:], A.add),
-         lambda: tt(T.oo[:, RIGHT], T.xt[:, 1], T.gs[:], A.subtract)],
+        + [lambda k=k: ts(T.mm[:, k], T.tt[:, min(k, 1), 1], (-3.0, 8.0, 8.0)[k], base[k] - 2 * D, A.mult, A.add) for k in range(3)],
+        [lambda: ts(T.gs[:], T.gg[:], float(X), -D, A.mult, A.add), lambda: ts(T.tt[:, 1, 0], T.tt[:, 1, 0], 7, None, A.bitwise_and)],
+        [lambda: tt(T.oo[:, LEFT], T.xt[:, 0], T.gs[:, 0], A.add), lambda: tt(T.oo[:, RIGHT], T.xt[:, 1], T.gs[:, 0], A.subtract),
+         lambda: tt(T.mm[:], T.mm[:], T.tt[:, :, 0], A.add)],
+        [lambda: tt(T.oo[:, LEFT], T.oo[:, LEFT], T.gs[:, 1], A.add), lambda: tt(T.mm[:, 1:3], T.mm[:, 1:3], T.gg[:], A.mult)],
         [lambda: tt(T.mm[:, 1], T.mm[:, 1], T.mm[:, 2], A.max)],
         [lambda: tt(T.oo[:, MID], T.mm[:, 0], T.mm[:, 1], A.max)],
-        [lambda d=d, a=a, b=b: ts(T.off[:, :, d:d + b - a], T.oo[:, :, a:b], float(X - 1), None, A.add) for d, a, b in runs],
+        [lambda d=d, a=a, b=b: ts(T.off[:, :, d:d + b - a], T.oo[:, :, a:b], 2 * D, None, A.add) for d, a, b in runs],
     ]
     at = {"step": 0, "e": [("dlo", 16), ("dln", 16)]}
 
@@ -226,20 +226,18 @@ def rank_program(g, core, T, topo):
     def scan_p(i, a=0, b=X):
         if a:
             vw(upto[i])
-        for n in (0, 1):
-            first = col(i, PT[n], a - 1, a) if a else 0.0
-            upto[i] = V(v.tensor_tensor_scan(col(i, PT[n], a, b), col(i, H0, a, b), T.cp[:, CP[n] + 2:CP[n] + 2 + b - a],
-                                             first, A.max, A.min))
+        first = col(i, P8, a - 1, a) if a else 0.0
+        upto[i] = V(v.tensor_tensor_scan(col(i, P8, a, b), col(i, H0, a, b), T.cp[:, 2:2 + b - a], first, A.max, A.min))
         return upto[i]
 
-    upto = {}
+    upto, e_six = {}, []
 
     def inner(i, k):
-        o = PAIR * (i // 2) + SEC * (i % 2) + C0 - k
+        o = PAIR * (i // 2) + X * (i % 2) + C0 - k
         return T.bt[:, o:o - X:-8]
 
     def middles(p):
-        i, o = 2 * p, PAIR * p + B12
+        i, o = 2 * p, PAIR * p
         vw(e_bz[p])
         for k in (i, i + 1):
             V(tt(inner(k, 6), col(k, H0, 1, X, 8), col(k, H0, 2, X, 8), A.max))
@@ -248,51 +246,51 @@ def rank_program(g, core, T, topo):
                 first = e
         vw(first)
         for k in (i, i + 1):
-            for n, b in enumerate(BL):
-                c = NG * (k - i) + 64 * n
-                f = V(tt(T.bm[:, p, c:c + X // b], col(k, PT[n], b - 3, X, b), col(k, H0, b - 2, X, b), A.max))
+            f = V(tt(T.bm[:, p, 64 * (k - i):64 * (k - i + 1)], col(k, P8, 5, X, 8), col(k, H0, 6, X, 8), A.max))
         vw(e)
         for k in (i, i + 1):
             V(tt(inner(k, 9), inner(k, 6), inner(k, 8), A.max))
+        need(g, "g", f)
+        e_six.append(G(g.affine_select(T.bt[:, o + B1 + 53:o + B2:64], T.bm[:, p, 6:NG:8], [[0, NG // 8]], A.is_equal, 0.0, 0, 0)))
         vw(f, e_cr)
-        for a in range(7):
-            e = V(v.tensor_tensor_scan(T.bt[:, o + a:o + 2 * SEC:8], T.bm[:, p], T.cr[:, 2 * NG * a:2 * NG * (a + 1)],
+        for n, (b, a) in enumerate([(B1, a) for a in range(5)] + [(B2, a) for a in range(7)]):
+            e = V(v.tensor_tensor_scan(T.bt[:, o + b + a:o + b + 2 * X:8], T.bm[:, p], T.cr[:, NG * n:NG * (n + 1)],
                                        0.0, A.max, A.min))
         return e
 
     def win(i, n):
         if n == MID:
             o = PAIR * (i // 2)
-            return T.bt[:, o + SEC * (i % 2):o + PAIR]
-        o = X * (H0 if n == LEFT else P64)
-        return T.tw[:, i, o:o + 3 * X]
+            return T.bt[:, o + X * (i % 2):o + PAIR]
+        return T.tw[:, i, X * H0:X * NT] if n == LEFT else T.tw[:, i, X * P8:X * S8]
 
     def off(n, j0, j1):
         return T.off[:, n, 6 * j0:6 * j1]
 
-    def gather(i, j0, j1, after, *ns):
-        w = WID[i // 2]
+    def gather(i, j0, j1, after, *ns, w=None):
+        w = w or WID[i // 2]
         for n in ns:
             aw(after, e_off)
             k = w * (i % 2) + min(n, w - 1)
-            e = S(act.activation(T.ga[:, i // 2, 2 * w * CAPP * j0 + k:2 * w * CAPP * j1:2 * w],
+            e = S(act.activation(T.ga[:, i // 2 * (w - 1), 2 * w * CAPP * j0 + k:2 * w * CAPP * j1:2 * w],
                                  win(i, n).indirect(off(n, j0, j1)), F.Copy))
         return e
 
-    def largest(p, j, e):
-        vw(e)
-        n = 2 * WID[p] * CAPP
-        mask, op = ((T.m3, A.min), (T.mi, A.mult))[p]
-        return V(v.tensor_tensor_scan(T.gb[:, p, n * j:n * j + n], mask[:], T.ga[:, p, n * j:n * j + n], 0.0, op, A.max))
+    def largest(p, j, e, w=None):
+        vw(e, e_m3)
+        w = w or WID[p]
+        n, p = 2 * w * CAPP, p * (w - 1)
+        mask, op = (T.m3, A.min) if w == 3 else (T.mi, A.mult)
+        return V(v.tensor_tensor_scan(T.gb[:, p, n * j:n * j + n], mask[:, 0:n], T.ga[:, p, n * j:n * j + n], 0.0, op, A.max))
 
     def take(j, e):
         need(g, "g", e)
         return G(g.affine_select(T.t[:, j, 0:4 * CAPP:2], T.gb[:, 0, 6 * CAPP * j + 2:6 * CAPP * (j + 1):3],
                                  [[0, 2 * CAPP]], A.is_equal, 0.0, 0, 0))
 
-    def copy3(j, e):
+    def copy3(j, e, p=0):
         vw(e)
-        return V(v.tensor_copy(T.t[:, j, 0:4 * CAPP:2], T.gb[:, 0, 6 * CAPP * j + 2:6 * CAPP * (j + 1):3]))
+        return V(v.tensor_copy(T.t[:, j, p:4 * CAPP:2], T.gb[:, 2 * p, 6 * CAPP * j + 2:6 * CAPP * (j + 1):3]))
 
     def second(buf, i, j):
         return buf[:, 1, 4 * CAPP * j + RES[i]:4 * CAPP * (j + 1):4]
@@ -305,44 +303,31 @@ def rank_program(g, core, T, topo):
 
     def codes(j, *es):
         vw(e_t, *es)
-        return quant(T.tq[:, 128 * j:128 * j + 128], T.tc[:, 128 * j:128 * j + 128], T.t[:, j])
+        return quant(T.tq[:, at_q(j):at_q(j) + 128], T.tc[:, at_q(j):at_q(j) + 128], T.t[:, j])
+
+    def at_q(j):
+        return 128 * ((j - cuts[0] - 1) % N)
 
     cuts = [(r - q - 1) % N for r in order(q)]
-    quant_a(0, 1)
-    h00 = make_h(0, 0, HALF, 0, quant_x(0, HALF, "dx0"))
-    index(IDX[0])
-    h10 = make_h(1, 0, HALF, 1, quant_a(1, 2))
-    index(IDX[1])
-    vw(e_cp, h00)
-    scan_p(0, 0, HALF)
-    index(1)
-    e = quant_x(HALF, X, "dx1")
-    h01 = make_h(0, HALF, X, 2, e)
-    h11 = make_h(1, HALF, X, 3, e)
-    index(1)
-    scan_s(0, 0, HALF)
-    index(1)
-    vw(h10)
-    scan_p(1, 0, HALF)
-    index(1)
-    if IDX[2]:
-        scan_s(1, 0, HALF)
-    index(9 - at["step"])
-    vw(h01)
-    e = scan_s(0, HALF, X)
-    e_off = index(1)
-    gather(0, 0, 3, e, LEFT)
-    e = scan_p(0, HALF, X)
-    gather(0, 0, 3, e, RIGHT)
-    e2 = quant_a(2, 4)
-    h2 = make_h(2, 0, X, 4, e2)
-    vw(h11)
-    e = scan_s(1, HALF if IDX[2] else 0, X)
-    gather(1, 0, 3, e, LEFT)
-    h3 = make_h(3, 0, X, 5, e2)
-    e = scan_p(1, HALF, X)
-    gather(1, 0, 3, e, RIGHT)
+    hs, got = {}, {}
+    for step in PLAN.split():
+        k, i, c = step[0], int(step[1]), step[2:]
+        if k == "i":
+            e_off = index(i)
+        elif k == "a":
+            e = quant_a(i, int(c or i) + 1)
+        elif k == "x":
+            e = quant_x(*part[str(i)], "dx%d" % i)
+        elif k == "h":
+            hs[i, c] = make_h(i, *part[c], len(hs), e)
+        elif k in "SP":
+            vw(e_cp, *[h for (r, d), h in hs.items() if r == i and part[d][0] < part[c][1] and part[c][0] < part[d][1]])
+            got[k, i] = (scan_s if k == "S" else scan_p)(i, *part[c])
+        else:
+            gather(i, 0, 3, got["S" if k == "L" else "P", i], LEFT if k == "L" else RIGHT)
+    h2, h3 = (max(h for (r, d), h in hs.items() if r == i) for i in (2, 3))
     e = middles(0)
+    aw(e_six[0])
     gather(0, 0, 3, e, MID)
     g0 = gather(1, 0, 3, e, MID)
     ends = {}
@@ -351,48 +336,55 @@ def rank_program(g, core, T, topo):
         es = scan_s(i)
         ends[i] = (es, scan_p(i))
     e_rows = middles(1)
+    vw(e_six[1])
     got = {}
     for js in (cuts[:1], sorted(cuts[1:])):
         for i in (2, 3):
             gather(i, js[0], js[-1] + 1, ends[i][0], LEFT)
             e = gather(i, js[0], js[-1] + 1, ends[i][1], RIGHT)
         got.update({j: e for j in js})
+    aw(e_six[1])
     own0 = [gather(i, 3, 4, e_rows, LEFT, MID, RIGHT) for i in (0, 1)][-1]
-    own1 = [gather(i, 3, 4, e_rows, LEFT, RIGHT) for i in (2, 3)][-1]
+    own = [gather(i, 3, 4, e_rows, *((LEFT, MID, RIGHT) if LATE else (LEFT, RIGHT)), w=2 + LATE) for i in (2, 3)][-1]
 
     def send(j, e):
-        r = (q + 1 + j) % N
-        k = order(q).index(r)
+        r, k = (q + 1 + j) % N, cuts.index(j)
         rid, pnc, _ = topo.addr(T.cores[r])
         need(g, "g", e)
-        for src, dst in ((T.tq[:, 128 * j:128 * j + CAPP].bitcast(dt.uint8), T.rq[:, CAPP * k:CAPP * (k + 1)].bitcast(dt.uint8)),
-                         (T.tc[:, 128 * j:128 * j + CAPP], T.rc[:, CAPP * k:CAPP * (k + 1)])):
-            g.remote_dma(dst, src, s.arrl if k == 2 else s.arre, s.loc, pnc, rid, topo.mask(core, T.cores[r]))
+        a, b = at_q(j), 512 + CAPP * k
+        for src, dst in ((T.tq[:, a:a + CAPP].bitcast(dt.uint8), T.tq[:, b:b + CAPP].bitcast(dt.uint8)),
+                         (T.tc[:, a:a + CAPP], T.tc[:, b:b + CAPP])):
+            g.remote_dma(dst, src, s["ar%d" % k], s.loc, pnc, rid, topo.mask(core, T.cores[r]))
 
     ja, jb, jc = cuts
     ta = take(ja, largest(0, ja, g0))
     a = largest(1, ja, got[ja])
     tb = take(jb, largest(0, jb, g0))
-    send(ja, codes(ja, joins(ja, a), ta))
+    e = joins(ja, a)
     c = largest(0, jc, g0)
+    send(ja, codes(ja, e, ta))
     b = largest(1, jb, got[jb])
-    vw(("gi", 32))
-    e_p = V(ts(T.offp[:], T.pp[:], 1, None, A.add))
+    copy3(jc, c)
     e = joins(jb, b)
-    c = largest(1, jc, got[jc]), c
+    c = largest(1, jc, got[jc])
     send(jb, codes(jb, e, tb))
-    joins(jc, c[0])
-    send(jc, codes(jc, copy3(jc, c[1])))
-    a = largest(0, 3, own0)
+    e = joins(jc, c)
+    vw(("gi", 96))
+    e_p = V(ts(T.offp[:], T.pp[:], 1, None, A.add))
+    send(jc, codes(jc, e))
     vw(("du", 16), ("dv", 16))
     e_uv = quant(T.uvq[:], T.uvc[:], T.uv[:])
-    b = largest(1, 3, own1)
+    a = largest(0, 3, own0)
+    b = largest(1, 3, own, 2 + LATE)
     copy3(3, a)
-    e_own = codes(3, joins(3, b))
+    e_own = codes(3, copy3(3, b, 1) if LATE else joins(3, b))
 
     def prod(x, xc, n, parts, bv, bu, both):
+        if both:
+            ev_ = mm(bv, n, T.uvq[:, 128:256], T.uvc[:, 128:256], x, xc)
         eu = mm(bu, n, T.uvq[:, 0:128], T.uvc[:, 0:128], x, xc)
-        ev_ = mm(bv, n, T.uvq[:, 128:256], T.uvc[:, 128:256], x, xc)
+        if not both:
+            ev_ = mm(bv, n, T.uvq[:, 128:256], T.uvc[:, 128:256], x, xc)
         for c, r in parts:
             aw(ev_)
             a = S(act.activation(T.zvs[:, CAPP * r + 1:CAPP * (r + 1) + 1], T.ps[:, 512 * bv + c:512 * bv + c + CAPP], F.Copy))
@@ -408,12 +400,18 @@ def rank_program(g, core, T, topo):
 
     frm = [[r for r in range(N) if r != q and order(r).index(q) == k][0] for k in range(3)]
     n_eng = [2 * len(topo.engines(T.cores[r], core)) for r in frm]
-    need(ten, "t", e_uv, h3, ("arre", n_eng[0] + n_eng[1]))
-    _, e_early = prod(T.rq[:, 0:192], T.rc[:, 0:192], 192, [(0, frm[0]), (CAPP, frm[1])], 0, 1, True)
+
+    def arrived(k, both):
+        need(ten, "t", ("ar%d" % k, n_eng[k]))
+        o = 480 + CAPP * k
+        return prod(T.tq[:, o:o + 128], T.tc[:, o:o + 128], 128, [(32, frm[k])], 2 * k, 2 * k + 1, both)
+
+    need(ten, "t", e_uv, h3)
+    arrived(0, True)
+    _, e_early = arrived(1, True)
     need(ten, "t", e_own)
-    prod(T.tq[:, 384:512], T.tc[:, 384:512], 128, [(0, q)], 2, 3, False)
-    need(ten, "t", ("arrl", n_eng[2]))
-    a, b = prod(T.rq[:, 160:288], T.rc[:, 160:288], 128, [(32, frm[2])], 4, 5, False)
+    prod(T.tq[:, at_q(3):at_q(3) + 128], T.tc[:, at_q(3):at_q(3) + 128], 128, [(0, q)], 6, 7, False)
+    a, b = arrived(2, False)
     aw(a, e_p)
     e = S(act.activation(T.y1[:, H:P], T.zvs[:].indirect(T.offp[:, H // 16:P // 16]), F.Copy))
     vw(b, e_early)

from concourse.bass import DstId, RemoteDMATransfer, IndirectOffsetOnAxis
from concourse.mybir import dt, AluOpType, ActivationFunctionType

A = AluOpType
F = ActivationFunctionType
N = 4
CAPP = 96
P = 256
SL = N * CAPP
X = 512
QUART, HALF = X // 4, X // 2
SH = (1, 3, 6)
BL = (8, 64)
P8, H0, S8, S64, NT = 0, 1, 2, 3, 4
ST = (S8, S64)
BIG = 1e29
NG = 2 * X // 8
C0 = 1041
Z0 = C0 - X - 1
B1 = Z0 + 2 * X
B2 = B1 + 2 * X
PAIR = B2 + 2 * X
LEFT, MID, RIGHT = 0, 1, 2
REM = 3 * CAPP
RES = (0, 2, 1, 3)
WID = (3, 2)
PLAN = "i3 a0 i1 x0 h00 i1 a1 h10 i1 x1 h01 h11 i1 P00 a2 h20 h21 i1 S00 a3 h30 h31 i1 S01 i1 P01 R0 L0 S1 P1 L1 R1"
LOADS = ("ln a0 a1 a2", "lo x0 x1 a3", "")
LATE = 0
H = 128

SCRATCH = {
    "xs": ("sbuf", [128, 2048], "bfloat16"),
    "ab": ("sbuf", [128, 2048], "bfloat16"),
    "uv": ("sbuf", [128, 1024], "bfloat16"),
    "xq": ("sbuf", [128, 512], "float8_e4m3fn_x4"),
    "xc": ("sbuf", [128, 512], "uint8"),
    "aq": ("sbuf", [128, 512], "float8_e4m3fn_x4"),
    "ac": ("sbuf", [128, 512], "uint8"),
    "uvq": ("sbuf", [128, 256], "float8_e4m3fn_x4"),
    "uvc": ("sbuf", [128, 256], "uint8"),
    "ps": ("psum", [128, 4096], "float32"),
    "tw": ("sbuf", [128, 4, NT * X], "bfloat16"),
    "bm": ("sbuf", [128, 2, NG], "bfloat16"),
    "bt": ("sbuf", [128, 2 * PAIR], "bfloat16"),
    "cp": ("sbuf", [128, 2 * X + 8], "bfloat16"),
    "cr": ("sbuf", [128, 12 * NG], "bfloat16"),
    "mi": ("sbuf", [128, 4 * CAPP], "bfloat16"),
    "m3": ("sbuf", [128, 7 * NG], "bfloat16"),
    "lnb": ("sbuf", [128, 24], "int32"),
    "xt": ("sbuf", [128, 2, 24], "int32"),
    "tt": ("sbuf", [128, 3, 2, 24], "int32"),
    "gg": ("sbuf", [128, 2, 24], "float32"),
    "gs": ("sbuf", [128, 2, 24], "float32"),
    "mm": ("sbuf", [128, 3, 24], "float32"),
    "oo": ("sbuf", [128, 3, 24], "float32"),
    "off": ("sbuf", [128, 3, 24], "uint16"),
    "ga": ("sbuf", [128, 3, 6 * SL], "bfloat16"),
    "gb": ("sbuf", [128, 3, 6 * SL], "bfloat16"),
    "t": ("sbuf", [128, N, 512], "bfloat16"),
    "tq": ("sbuf", [128, 512 + REM], "float8_e4m3fn_x4"),
    "tc": ("sbuf", [128, 512 + REM], "uint8"),
    "pidx": ("sbuf", [128, 1], "int32"),
    "pid16": ("sbuf", [128, 1], "int32"),
    "pp": ("sbuf", [128, 32], "int32"),
    "offp": ("sbuf", [128, 32], "uint16"),
    "zvs": ("sbuf", [128, SL + 1], "float32"),
    "zus": ("sbuf", [128, SL + 1], "float32"),
    "y1": ("sbuf", [128, P], "float32"),
    "ys": ("sbuf", [128, P], "float32"),
}
SEMAPHORES = ["sv", "st", "sa", "sg", "dlo", "dln", "dx0", "dx1", "dx2", "dx3", "dx4", "dx5", "dx6", "da0", "da1", "da2", "da3", "du", "dv", "dy",
              "gi", "ar0", "ar1", "ar2", "loc"]


def rank_program(g, core, T, topo):
    q = T.rank_of(core)
    if q is None:
        return
    v, ten, act, sy, s = g.vector, g.tensor, g.scalar, g.sync, T.sem
    cnt = {"sv": 0, "st": 0, "sa": 0, "sg": 0}
    seen = {}

    def done(ins, name):
        cnt[name] += 1
        ins.then_inc(s[name], 1)
        return (name, cnt[name])

    def need(eng, en, *evs):
        for name, val in evs:
            if seen.get((en, name), 0) < val:
                eng.wait_ge(s[name], val)
                seen[(en, name)] = val

    def V(ins):
        return done(ins, "sv")

    def S(ins):
        return done(ins, "sa")

    def G(ins):
        return done(ins, "sg")

    def vw(*evs):
        need(v, "v", *evs)

    def aw(*evs):
        need(act, "a", *evs)

    def order(r):
        far = [(r + 1 + j) % N for j in range(N - 1)]
        return sorted(far, key=lambda k: topo.same_plane(topo.chip(T.cores[r]), topo.chip(T.cores[k])))

    def load_a(eng, i):
        eng.dma_start(T.ab[:, 512 * i:512 * i + 512], T.a[:, 512 * RES[i]:512 * RES[i] + 512]).then_inc(s["da%d" % i], 16)

    def load_x(a, b, sem):
        sy.dma_start(T.xs[:, 4 * a:4 * b], T.x[:, 4 * a:4 * b]).then_inc(sem, 16)

    part = {"0": (0, HALF), "1": (HALF, X), "": (0, X), "2": (0, QUART), "3": (QUART, HALF), "4": (QUART, X),
            "5": (HALF, HALF + QUART), "6": (HALF + QUART, X)}
    for eng, names in zip((act, sy, g), LOADS):
        for name in names.split():
            if name == "ln":
                eng.dma_start(T.lnb[:], T.ln[:]).then_inc(s.dln, 16)
            elif name == "lo":
                eng.dma_start(T.xt[:, 0], T.lo[:]).then_inc(s.dlo, 16)
            elif name[0] == "a":
                load_a(eng, int(name[1]))
            else:
                a, b = part[name[1]]
                eng.dma_start(T.xs[:, 4 * a:4 * b], T.x[:, 4 * a:4 * b]).then_inc(s["d" + name], 16)
    sy.dma_start(T.uv[:, 0:512], T.u[:]).then_inc(s.du, 16)
    sy.dma_start(T.uv[:, 512:1024], T.v[:]).then_inc(s.dv, 16)
    for k in range(4):
        sy.dma_start(T.pp[16 * (k // 2):16 * (k // 2) + 16, 16 * (k % 2):16 * (k % 2) + 16], (T.pf, T.pg)[k % 2][:]).then_inc(s.gi, 16)
    for k, n in enumerate((32, 64)):
        sy.wait_ge(s.gi, 64 + 16 * k)
        sy.dma_start(T.pp[n:2 * n], T.pp[0:n]).then_inc(s.gi, 16)

    CP = (0, X + 8)
    e_big = V(v.memset(T.m3[:], BIG))
    e = V(v.memset(T.cp[:], BIG))
    V(v.memset(T.zus[:, 0:1], 0.0))
    vw(e)
    for n, b in enumerate(BL):
        e_cp = V(v.memset(T.cp[:, CP[n]:CP[n] + X + 8 - 8 * n:b], 0.0))
    aw(e_cp)
    e_bz = [S(act.activation(T.bt[:, PAIR * p + Z0:PAIR * p + B1:2], T.cp[:, 0:X], F.Copy, scale=0.0)) for p in (0, 1)]
    e_t = S(act.activation(T.t[:, :, 4 * CAPP:512], T.cp[:, 0:X], F.Copy, scale=0.0))

    def fill(out, pattern):
        return G(g.iota(out, pattern, 0, 0, allow_small_or_imprecise_dtypes=True))

    need(g, "g", e_big)
    G(g.affine_select(T.cr[:, 0:5 * NG], T.m3[:, 0:5 * NG], [[-1, 5], [0, NG // 8], [1, 8]], A.is_gt, 0.0, 0, 0))
    e_cr = G(g.affine_select(T.cr[:, 5 * NG:12 * NG], T.m3[:], [[-8, 7], [0, 2], [1, NG // 2]], A.is_ge, 0.0, -8, 0))
    for o in (0, PAIR):
        fill(T.bt[:, o + B1 + 45:o + B2:64], [[0, NG // 8]])
        fill(T.bt[:, o + B1 + 54:o + B2:64], [[0, NG // 8]])
        fill(T.bt[:, o + B1 + 7:o + PAIR:8], [[0, 2 * NG]])
    fill(T.mi[:], [[0, 2 * CAPP], [1, 2]])
    need(g, "g", e_cr)
    e_m3 = fill(T.m3[:, 0:6 * CAPP:3], [[0, 2 * CAPP]])

    m = 6 * ((q + 1) % N)
    runs = [(0, m, 24)] + ([(24 - m, 0, m)] if m else [])
    ts, tt = v.tensor_scalar, v.tensor_tensor
    base = (C0, B1 - 8, B2 - 8)
    D = (X - 2) / 3.0
    steps = [
        [lambda: tt(T.xt[:, 1], T.xt[:, 0], T.lnb[:], A.add)],
        [lambda: ts(T.xt[:, 1], T.xt[:, 1], 1, None, A.add)],
        [lambda k=k: ts(T.tt[:, k], T.xt[:], SH[k], None, A.arith_shift_right) for k in (1, 2, 0)],
        [lambda: tt(T.gg[:], T.tt[:, 1:3, 1], T.tt[:, 1:3, 0], A.is_gt)]
        + [lambda k=k: ts(T.mm[:, k], T.tt[:, min(k, 1), 1], (-3.0, 8.0, 8.0)[k], base[k] - 2 * D, A.mult, A.add) for k in range(3)],
        [lambda: ts(T.gs[:], T.gg[:], float(X), -D, A.mult, A.add), lambda: ts(T.tt[:, 1, 0], T.tt[:, 1, 0], 7, None, A.bitwise_and)],
        [lambda: tt(T.oo[:, LEFT], T.xt[:, 0], T.gs[:, 0], A.add), lambda: tt(T.oo[:, RIGHT], T.xt[:, 1], T.gs[:, 0], A.subtract),
         lambda: tt(T.mm[:], T.mm[:], T.tt[:, :, 0], A.add)],
        [lambda: tt(T.oo[:, LEFT], T.oo[:, LEFT], T.gs[:, 1], A.add), lambda: tt(T.mm[:, 1:3], T.mm[:, 1:3], T.gg[:], A.mult)],
        [lambda: tt(T.mm[:, 1], T.mm[:, 1], T.mm[:, 2], A.max)],
        [lambda: tt(T.oo[:, MID], T.mm[:, 0], T.mm[:, 1], A.max)],
        [lambda d=d, a=a, b=b: ts(T.off[:, :, d:d + b - a], T.oo[:, :, a:b], 2 * D, None, A.add) for d, a, b in runs],
    ]
    at = {"step": 0, "e": [("dlo", 16), ("dln", 16)]}

    def index(n):
        for _ in range(n):
            vw(*at["e"])
            for call in steps[at["step"]]:
                at["e"] = [V(call())]
            at["step"] += 1
        return at["e"][0]

    def quant(dst, sc, src):
        return V(v.quantize_mx(dst, sc, src))

    def mm(bank, n, w, wc, x, xc):
        return done(ten.matmul_mx(T.ps[:, 512 * bank:512 * bank + n], w, wc, x, xc, True, True), "st")

    def col(i, t, a=0, b=X, st=1):
        return T.tw[:, i, X * t + a:X * t + b:st]

    def back(i, t, a, b):
        return T.tw[:, i, X * t + b - 1:X * t + a - 1:-1]

    def make_h(i, a, b, bank, e):
        need(ten, "t", e)
        z = mm(bank, b - a, T.aq[:, 128 * i:128 * i + 128], T.ac[:, 128 * i:128 * i + 128], T.xq[:, a:b], T.xc[:, a:b])
        aw(z)
        return S(act.activation(col(i, H0, a, b), T.ps[:, 512 * bank:512 * bank + b - a], F.Relu, scale=0.05))

    def quant_a(i0, i1):
        vw(*[("da%d" % i, 16) for i in range(i0, i1)])
        return quant(T.aq[:, 128 * i0:128 * i1], T.ac[:, 128 * i0:128 * i1], T.ab[:, 512 * i0:512 * i1])

    def quant_x(a, b, sem):
        vw((sem, 16))
        return quant(T.xq[:, a:b], T.xc[:, a:b], T.xs[:, 4 * a:4 * b])

    def scan_s(i, a=0, b=X):
        for n in (0, 1):
            e = V(v.tensor_tensor_scan(back(i, ST[n], a, b), back(i, H0, a, b), T.cp[:, CP[n]:CP[n] + b - a], 0.0, A.max, A.min))
        return e

    def scan_p(i, a=0, b=X):
        if a:
            vw(upto[i])
        first = col(i, P8, a - 1, a) if a else 0.0
        upto[i] = V(v.tensor_tensor_scan(col(i, P8, a, b), col(i, H0, a, b), T.cp[:, 2:2 + b - a], first, A.max, A.min))
        return upto[i]

    upto, e_six = {}, []

    def inner(i, k):
        o = PAIR * (i // 2) + X * (i % 2) + C0 - k
        return T.bt[:, o:o - X:-8]

    def middles(p):
        i, o = 2 * p, PAIR * p
        vw(e_bz[p])
        for k in (i, i + 1):
            V(tt(inner(k, 6), col(k, H0, 1, X, 8), col(k, H0, 2, X, 8), A.max))
            e = V(tt(inner(k, 8), col(k, H0, 3, X, 8), col(k, H0, 4, X, 8), A.max))
            if k == i:
                first = e
        vw(first)
        for k in (i, i + 1):
            f = V(tt(T.bm[:, p, 64 * (k - i):64 * (k - i + 1)], col(k, P8, 5, X, 8), col(k, H0, 6, X, 8), A.max))
        vw(e)
        for k in (i, i + 1):
            V(tt(inner(k, 9), inner(k, 6), inner(k, 8), A.max))
        need(g, "g", f)
        e_six.append(G(g.affine_select(T.bt[:, o + B1 + 53:o + B2:64], T.bm[:, p, 6:NG:8], [[0, NG // 8]], A.is_equal, 0.0, 0, 0)))
        vw(f, e_cr)
        for n, (b, a) in enumerate([(B1, a) for a in range(5)] + [(B2, a) for a in range(7)]):
            e = V(v.tensor_tensor_scan(T.bt[:, o + b + a:o + b + 2 * X:8], T.bm[:, p], T.cr[:, NG * n:NG * (n + 1)],
                                       0.0, A.max, A.min))
        return e

    def win(i, n):
        if n == MID:
            o = PAIR * (i // 2)
            return T.bt[:, o + X * (i % 2):o + PAIR]
        return T.tw[:, i, X * H0:X * NT] if n == LEFT else T.tw[:, i, X * P8:X * S8]

    def off(n, j0, j1):
        return T.off[:, n, 6 * j0:6 * j1]

    def gather(i, j0, j1, after, *ns, w=None):
        w = w or WID[i // 2]
        for n in ns:
            aw(after, e_off)
            k = w * (i % 2) + min(n, w - 1)
            e = S(act.activation(T.ga[:, i // 2 * (w - 1), 2 * w * CAPP * j0 + k:2 * w * CAPP * j1:2 * w],
                                 win(i, n).indirect(off(n, j0, j1)), F.Copy))
        return e

    def largest(p, j, e, w=None):
        vw(e, e_m3)
        w = w or WID[p]
        n, p = 2 * w * CAPP, p * (w - 1)
        mask, op = (T.m3, A.min) if w == 3 else (T.mi, A.mult)
        return V(v.tensor_tensor_scan(T.gb[:, p, n * j:n * j + n], mask[:, 0:n], T.ga[:, p, n * j:n * j + n], 0.0, op, A.max))

    def take(j, e):
        need(g, "g", e)
        return G(g.affine_select(T.t[:, j, 0:4 * CAPP:2], T.gb[:, 0, 6 * CAPP * j + 2:6 * CAPP * (j + 1):3],
                                 [[0, 2 * CAPP]], A.is_equal, 0.0, 0, 0))

    def copy3(j, e, p=0):
        vw(e)
        return V(v.tensor_copy(T.t[:, j, p:4 * CAPP:2], T.gb[:, 2 * p, 6 * CAPP * j + 2:6 * CAPP * (j + 1):3]))

    def second(buf, i, j):
        return buf[:, 1, 4 * CAPP * j + RES[i]:4 * CAPP * (j + 1):4]

    def joins(j, e):
        vw(e)
        for i in (2, 3):
            e = V(tt(T.t[:, j, RES[i]:4 * CAPP:4], win(i, MID).indirect(off(MID, j, j + 1)), second(T.gb, i, j), A.max))
        return e

    def codes(j, *es):
        vw(e_t, *es)
        return quant(T.tq[:, at_q(j):at_q(j) + 128], T.tc[:, at_q(j):at_q(j) + 128], T.t[:, j])

    def at_q(j):
        return 128 * ((j - cuts[0] - 1) % N)

    cuts = [(r - q - 1) % N for r in order(q)]
    hs, got = {}, {}
    for step in PLAN.split():
        k, i, c = step[0], int(step[1]), step[2:]
        if k == "i":
            e_off = index(i)
        elif k == "a":
            e = quant_a(i, int(c or i) + 1)
        elif k == "x":
            e = quant_x(*part[str(i)], "dx%d" % i)
        elif k == "h":
            hs[i, c] = make_h(i, *part[c], len(hs), e)
        elif k in "SP":
            vw(e_cp, *[h for (r, d), h in hs.items() if r == i and part[d][0] < part[c][1] and part[c][0] < part[d][1]])
            got[k, i] = (scan_s if k == "S" else scan_p)(i, *part[c])
        else:
            gather(i, 0, 3, got["S" if k == "L" else "P", i], LEFT if k == "L" else RIGHT)
    h2, h3 = (max(h for (r, d), h in hs.items() if r == i) for i in (2, 3))
    e = middles(0)
    aw(e_six[0])
    gather(0, 0, 3, e, MID)
    g0 = gather(1, 0, 3, e, MID)
    ends = {}
    for i, h in ((2, h2), (3, h3)):
        vw(h)
        es = scan_s(i)
        ends[i] = (es, scan_p(i))
    e_rows = middles(1)
    vw(e_six[1])
    got = {}
    for js in (cuts[:1], sorted(cuts[1:])):
        for i in (2, 3):
            gather(i, js[0], js[-1] + 1, ends[i][0], LEFT)
            e = gather(i, js[0], js[-1] + 1, ends[i][1], RIGHT)
        got.update({j: e for j in js})
    aw(e_six[1])
    own0 = [gather(i, 3, 4, e_rows, LEFT, MID, RIGHT) for i in (0, 1)][-1]
    own = [gather(i, 3, 4, e_rows, *((LEFT, MID, RIGHT) if LATE else (LEFT, RIGHT)), w=2 + LATE) for i in (2, 3)][-1]

    def send(j, e):
        r, k = (q + 1 + j) % N, cuts.index(j)
        rid, pnc, _ = topo.addr(T.cores[r])
        need(g, "g", e)
        a, b = at_q(j), 512 + CAPP * k
        for src, dst in ((T.tq[:, a:a + CAPP].bitcast(dt.uint8), T.tq[:, b:b + CAPP].bitcast(dt.uint8)),
                         (T.tc[:, a:a + CAPP], T.tc[:, b:b + CAPP])):
            g.remote_dma(dst, src, s["ar%d" % k], s.loc, pnc, rid, topo.mask(core, T.cores[r]))

    ja, jb, jc = cuts
    ta = take(ja, largest(0, ja, g0))
    a = largest(1, ja, got[ja])
    tb = take(jb, largest(0, jb, g0))
    e = joins(ja, a)
    c = largest(0, jc, g0)
    send(ja, codes(ja, e, ta))
    b = largest(1, jb, got[jb])
    copy3(jc, c)
    e = joins(jb, b)
    c = largest(1, jc, got[jc])
    send(jb, codes(jb, e, tb))
    e = joins(jc, c)
    vw(("gi", 96))
    e_p = V(ts(T.offp[:], T.pp[:], 1, None, A.add))
    send(jc, codes(jc, e))
    vw(("du", 16), ("dv", 16))
    e_uv = quant(T.uvq[:], T.uvc[:], T.uv[:])
    a = largest(0, 3, own0)
    b = largest(1, 3, own, 2 + LATE)
    copy3(3, a)
    e_own = codes(3, copy3(3, b, 1) if LATE else joins(3, b))

    def prod(x, xc, n, parts, bv, bu, both):
        if both:
            ev_ = mm(bv, n, T.uvq[:, 128:256], T.uvc[:, 128:256], x, xc)
        eu = mm(bu, n, T.uvq[:, 0:128], T.uvc[:, 0:128], x, xc)
        if not both:
            ev_ = mm(bv, n, T.uvq[:, 128:256], T.uvc[:, 128:256], x, xc)
        for c, r in parts:
            aw(ev_)
            a = S(act.activation(T.zvs[:, CAPP * r + 1:CAPP * (r + 1) + 1], T.ps[:, 512 * bv + c:512 * bv + c + CAPP], F.Copy))
        for c, r in parts:
            to, fr = T.zus[:, CAPP * r + 1:CAPP * (r + 1) + 1], T.ps[:, 512 * bu + c:512 * bu + c + CAPP]
            if both:
                aw(eu)
                b = S(act.activation(to, fr, F.Copy))
            else:
                vw(eu)
                b = V(v.tensor_copy(to, fr))
        return a, b

    frm = [[r for r in range(N) if r != q and order(r).index(q) == k][0] for k in range(3)]
    n_eng = [2 * len(topo.engines(T.cores[r], core)) for r in frm]

    def arrived(k, both):
        need(ten, "t", ("ar%d" % k, n_eng[k]))
        o = 480 + CAPP * k
        return prod(T.tq[:, o:o + 128], T.tc[:, o:o + 128], 128, [(32, frm[k])], 2 * k, 2 * k + 1, both)

    need(ten, "t", e_uv, h3)
    arrived(0, True)
    _, e_early = arrived(1, True)
    need(ten, "t", e_own)
    prod(T.tq[:, at_q(3):at_q(3) + 128], T.tc[:, at_q(3):at_q(3) + 128], 128, [(0, q)], 6, 7, False)
    a, b = arrived(2, False)
    aw(a, e_p)
    e = S(act.activation(T.y1[:, H:P], T.zvs[:].indirect(T.offp[:, H // 16:P // 16]), F.Copy))
    vw(b, e_early)
    f = V(v.tensor_copy(T.y1[:, 0:H], T.zus[:].indirect(T.offp[:, P // 16:(P + H) // 16])))
    for c, d, eng, en in ((0, H, sy, "s"), (H, P, act, "a")):
        vw(*((e,) if c else (f, a)))
        w, k = (T.zus, P) if c else (T.zvs, 0)
        o = V(tt(T.ys[:, c:d], w[:].indirect(T.offp[:, (k + c) // 16:(k + d) // 16]), T.y1[:, c:d], A.add))
        need(eng, en, o)
        eng.dma_start(T.y[:, c:d], T.ys[:, c:d]).then_inc(s.dy, 16)
    sy.wait_ge(s.dy, 32)
    g.wait_ge(s.loc, sum(2 * len(topo.engines(core, T.cores[r])) for r in order(q)))
    for name in ("sv", "st", "sa", "sg"):
        need(g, "g", (name, cnt[name]))
